import numpy as np
import ml_dtypes


def mxq(x, axis, fmt="e4m3"):
    dtype, down = {"e4m3": (ml_dtypes.float8_e4m3fn, 7), "e5m2": (ml_dtypes.float8_e5m2, 14)}[fmt]
    v = np.moveaxis(np.asarray(x, np.float32).astype(ml_dtypes.bfloat16).astype(np.float64), axis, -1)
    blocks = v.reshape(v.shape[:-1] + (-1, 32))
    amax = np.abs(blocks).max(-1, keepdims=True)
    byte = np.maximum(np.where(amax > 0, np.frexp(amax)[1] - 1 + 127, 0) - down, 1)
    scale = np.exp2(byte - 127.0)
    codes = (blocks / scale).astype(np.float32).astype(dtype).astype(np.float64)
    return np.moveaxis((codes * scale).reshape(v.shape), -1, axis)


WIDE = False


def mx_kscale(k):
    if not WIDE:
        return np.ones(k)
    levels = np.array([24, -24, 12, -12, 0])
    if k % 512:
        return np.exp2(np.random.permutation(np.resize(levels, k // 32))).repeat(32)
    a = np.empty((k // 512, 16))
    for p in range(k // 512):
        a[p, :8] = np.random.permutation(np.resize(levels, 8))
        for g in range(8):
            far = levels[np.abs(levels - a[p, g]) >= 10]
            a[p, g + 8] = far[np.random.randint(len(far))]
    return np.exp2(a.ravel()).repeat(32)


def f64(x):
    return np.asarray(x).astype(np.float64)


def striped(idx):
    return np.tile(idx.reshape(-1, 16).T, (8, 1)).astype(np.uint16)


def unstriped(offs):
    return offs[:16].T.reshape(-1).astype(np.int64)


E2M1 = np.array([0.0, 0.5, 1.0, 1.5, 2.0, 3.0, 4.0, 6.0, -0.0, -0.5, -1.0, -1.5, -2.0, -3.0, -4.0, -6.0])


def pack_weight(w, fmt):
    k, n = w.shape
    w = f64(np.asarray(w, np.float32).astype(ml_dtypes.bfloat16)).reshape(k // 32, 32, n)
    amax = np.abs(w).max(1)
    if fmt == "e4m3":
        byte = np.frexp(amax)[1] - 1 + 127 - 7
    else:
        mant, ex = np.frexp(amax / 6.0)
        byte = np.where(mant > 0.5, ex, ex - 1) + 127
    byte = np.clip(np.where(amax > 0, byte, 1), 1, 254)
    scaled = (w * np.exp2(127.0 - byte)[:, None, :]).reshape(k, n).astype(np.float32)
    by_word = np.ascontiguousarray(scaled.reshape(k // 512, 128, 4, n).transpose(0, 1, 3, 2))
    if fmt == "e4m3":
        words = by_word.astype(ml_dtypes.float8_e4m3fn).view(np.uint8)
    else:
        c = by_word.astype(ml_dtypes.float4_e2m1fn).view(np.uint8) & 0xF
        words = (c[..., 0::2] | (c[..., 1::2] << 4)).reshape(k // 512, 128, 2 * n)
    return np.ascontiguousarray(words), np.ascontiguousarray(byte.astype(np.uint8).reshape(k // 512, 16, n))


def unpack_weight(words, scales, fmt):
    g, _, n = scales.shape
    words = np.ascontiguousarray(words).reshape(g, 128, n, -1)
    if fmt == "e4m3":
        vals = words.view(ml_dtypes.float8_e4m3fn).astype(np.float64)
    else:
        nib = np.empty((g, 128, n, 4), np.uint8)
        nib[..., 0::2] = words & 0xF
        nib[..., 1::2] = words >> 4
        vals = E2M1[nib]
    vals = vals * np.repeat(np.exp2(scales.astype(np.float64) - 127.0), 8, axis=1)[..., None]
    return vals.transpose(0, 1, 3, 2).reshape(g * 512, n)


def pack_table4(v):
    words, scales = pack_weight(v, "e2m1")
    g, t = words.shape[0] // 2, v.shape[1]
    return np.ascontiguousarray(words.reshape(g, 2, 128, t, 2).transpose(0, 2, 3, 1, 4).reshape(g, 128, t, 4)), scales


def unpack_table4(words, scales):
    g, _, t, _ = words.shape
    return unpack_weight(words.reshape(g, 128, t, 2, 2).transpose(0, 3, 1, 2, 4).reshape(2 * g, 128, 2 * t), scales, "e2m1")


def sigm(f):
    return 1.0 / (1.0 + np.exp(-np.maximum(f, -700.0)))


K, N, T, J = 1024, 1024, 4096, 2048


def setup_inputs():
    n = np.random.standard_normal
    s = mx_kscale(K)[:, None]
    wv = n((K, N)) / np.sqrt(K) / s
    p_tab = pack_table4(n((K, T)) * s)
    p_wk = pack_weight(n((K, N)) / np.sqrt(K) / s, "e4m3")
    p_wv4 = pack_weight(wv[512:], "e2m1")
    return {
        "tab_words": p_tab[0],
        "tab_scales": p_tab[1],
        "wk_words": p_wk[0],
        "wk_scales": p_wk[1],
        "wv8": (wv[:512]).astype(np.float32),
        "wv4_words": p_wv4[0],
        "wv4_scales": p_wv4[1],
        "st": (n((N, J))).astype(np.float32),
        "rT": (n((N, T))).astype(np.float32),
        "offs": striped(np.random.permutation(T)[:J]),
    }


def reference(tab_words, tab_scales, wk_words, wk_scales, wv8, wv4_words, wv4_scales, st, rT, offs):
    idx = unstriped(offs)
    tab_ = unpack_table4(tab_words, tab_scales)[:, idx]
    wk_ = unpack_weight(wk_words, wk_scales, "e4m3")
    wv8_ = mxq(f64(wv8), 0, "e4m3")
    wv4_ = unpack_weight(wv4_words, wv4_scales, "e2m1")
    ke = wk_.T @ tab_
    ve = wv8_.T @ tab_[:512] + wv4_.T @ tab_[512:]
    gate = sigm(ke * f64(st))
    return f64(rT)[:, idx] + gate * ve

@@ -1,0 +1,200 @@
+from contextlib import ExitStack
+
+import concourse.mybir as mybir
+
+K, N, T, J = 1024, 1024, 4096, 2048
+FLOPS = 2 * 2 * K * N * J
+
+F32 = mybir.dt.float32
+BF16 = mybir.dt.bfloat16
+I32 = mybir.dt.int32
+U32 = mybir.dt.uint32
+U16 = mybir.dt.uint16
+U8 = mybir.dt.uint8
+FP8X4 = mybir.dt.float8_e4m3fn_x4
+FP4X4 = mybir.dt.float4_e2m1fn_x4
+MULT = mybir.AluOpType.mult
+ADD = mybir.AluOpType.add
+SIGMOID = mybir.ActivationFunctionType.Sigmoid
+
+P = 128
+PACK = 4
+QUADS = 4
+ROWS = 4
+CHUNK = 512
+CHUNKS = J // CHUNK
+TILES = N // P
+HALF = N // 2
+QUANT = 256
+LIST_COLS = J // 16
+
+
+def tile_list_engram_qf_sigL_kernel(
+    tc, tab_words, tab_scales, wk_words, wk_scales, wv8, wv4_words, wv4_scales, st, rT, offs, out
+):
+    nc = tc.nc
+    with ExitStack() as ctx:
+        held = ctx.enter_context(tc.tile_pool(name="held", bufs=1))
+        psum = ctx.enter_context(tc.psum_pool(name="psum", bufs=CHUNKS))
+
+        offsets = held.tile([P, LIST_COLS], U16, name="offsets")
+        nc.sync.dma_start(offsets[:], offs)
+
+        tab_s = held.tile([P, T], U8, name="tab_s", tag="work4", align_bytes=64)
+        nc.sync.dma_start(out=tab_s[0:32, :].bitcast(I32), in_=tab_scales.rearrange("a q t -> (a q) t").bitcast(I32))
+        nc.vector.memset(tab_s[32:64, :].bitcast(I32), 0)
+        nc.vector.memset(tab_s[64:128, :].bitcast(I32), 0)
+        tab_w = held.tile([P, T], U32, name="tab_w", tag="work1", align_bytes=64)
+        nc.sync.dma_start(out=tab_w[:].bitcast(I32), in_=tab_words[0].rearrange("p t b -> p (t b)").bitcast(I32))
+
+        warm = held.tile([P, 8], F32, name="warm")
+        nc.gpsimd.memset(warm[:], 0.0)
+        nc.scalar.activation(warm[:], warm[:], SIGMOID)
+
+        w_s = held.tile([P, 3, N], U8, name="w_s", align_bytes=64)
+        nc.gpsimd.memset(w_s[:].rearrange("p a n -> p (a n)").bitcast(I32), 0)
+        v_s = held.tile([P, 2, J], U8, name="v_s", align_bytes=64)
+        nc.gpsimd.memset(v_s[:].rearrange("p a j -> p (a j)").bitcast(I32), 0)
+
+        wv8_rows = wv8.rearrange("(p i) n -> p i n", i=PACK)
+        wk_rows = wk_words.rearrange("a p n b -> p a (n b)")
+
+        def load_wv8(h, tag):
+            raw = held.tile([P, PACK, HALF], F32, name="raw", tag=tag, align_bytes=64)
+            nc.sync.dma_start(out=raw[:], in_=wv8_rows[:, :, h * HALF : (h + 1) * HALF])
+            return raw
+
+        def load_wk(h, tag):
+            words = held.tile([P, 2, HALF], U32, name="words", tag=tag, align_bytes=64)
+            nc.sync.dma_start(
+                out=words[:].bitcast(I32), in_=wk_rows[:, :, 4 * h * HALF : 4 * (h + 1) * HALF].bitcast(I32)
+            )
+            return words
+
+        def load_st(i):
+            work = held.tile([P, J], F32, name="work", tag=f"work{i % 5}", align_bytes=64)
+            nc.sync.dma_start(out=work[:], in_=st[i * P : (i + 1) * P, :])
+            return work
+
+        wv8_raw = [load_wv8(0, "record0")]
+        wk_w = [load_wk(0, "wk0")]
+        for q in range(QUADS):
+            nc.scalar.dma_start(
+                out=w_s[32 * q : 32 * q + ROWS, 0:2, :].bitcast(I32),
+                in_=wk_scales[:, ROWS * q : ROWS * (q + 1), :].rearrange("a r n -> r a n").bitcast(I32),
+            )
+        for q in range(QUADS):
+            nc.scalar.dma_start(
+                out=w_s[32 * q : 32 * q + ROWS, 2, :].bitcast(I32),
+                in_=wv4_scales[0, ROWS * q : ROWS * (q + 1), :].bitcast(I32),
+            )
+        wv4_w = held.tile([P, 2 * N], U8, name="wv4_w", align_bytes=64)
+        nc.sync.dma_start(out=wv4_w[:].bitcast(I32), in_=wv4_words[0].bitcast(I32))
+
+        picked_s = held.tile([P, J], U8, name="picked_s", tag="wk1", align_bytes=64)
+        nc.vector.tensor_copy(picked_s[:], tab_s[:].indirect(offsets[:]))
+        for a in range(2):
+            for q in range(QUADS):
+                row = 16 * a + ROWS * q
+                nc.scalar.dma_start(
+                    out=v_s[32 * q : 32 * q + ROWS, a, :].bitcast(I32),
+                    in_=picked_s[row : row + ROWS, :].bitcast(I32),
+                )
+        wv8_raw.append(load_wv8(1, "work4"))
+        v_w = held.tile([P, 2, 2 * J], U8, name="v_w", align_bytes=64)
+        picked_w = []
+        for h, tag in enumerate(("record1", "work2")):
+            picked = held.tile([P, J // 2], U32, name="picked", tag=tag, align_bytes=64)
+            nc.vector.tensor_copy(
+                picked[:], tab_w[:].indirect(offsets[:, h * LIST_COLS // 2 : (h + 1) * LIST_COLS // 2])
+            )
+            picked_w.append(picked)
+        for h in range(2):
+            nc.vector.tensor_copy(
+                v_w[:].bitcast(U16)[:, :, h * J // 2 : (h + 1) * J // 2],
+                picked_w[h][:].bitcast(U16).rearrange("p (j d) -> p d j", d=2),
+            )
+        wk_w.append(load_wk(1, "wk1"))
+
+        wv8_w = held.tile([P, N], U32, name="wv8_w", align_bytes=64)
+        wv8_s = held.tile([P, N], U8, name="wv8_s", align_bytes=64)
+        for h, tag in enumerate(("record2", "work3")):
+            grouped = held.tile([P, HALF, PACK], BF16, name="grouped", tag=tag, align_bytes=64)
+            for c0 in range(0, HALF, QUANT):
+                n0 = h * HALF + c0
+                nc.scalar.copy(
+                    grouped[:, c0 : c0 + QUANT, :], wv8_raw[h][:, :, c0 : c0 + QUANT].rearrange("p i n -> p n i")
+                )
+                nc.vector.quantize_mx(
+                    out=wv8_w[:, n0 : n0 + QUANT].bitcast(FP8X4),
+                    scales=wv8_s[:, n0 : n0 + QUANT],
+                    in_=grouped[:, c0 : c0 + QUANT, :].rearrange("p n i -> p (n i)"),
+                )
+
+        def moving(a, c):
+            return dict(
+                rhs=v_w[:, a, 2 * c * CHUNK : 2 * (c + 1) * CHUNK].bitcast(FP4X4),
+                rhs_scale=v_s[:, a, c * CHUNK : (c + 1) * CHUNK],
+            )
+
+        for i in range(TILES):
+            rows = slice(i * P, (i + 1) * P)
+            work = load_st(i)
+            record = held.tile([P, T], F32, name="record", tag=f"record{i % 3}", align_bytes=64)
+            nc.sync.dma_start(out=record[:], in_=rT[rows, :])
+
+            c0 = (i * P) % HALF
+            ke, ve = [], []
+            for c in range(CHUNKS):
+                bank = psum.tile([P, CHUNK], F32, name="ke")
+                for a in range(2):
+                    nc.tensor.matmul_mx(
+                        out=bank[:],
+                        lhsT=wk_w[i * P // HALF][:, a, c0 : c0 + P].bitcast(FP8X4),
+                        lhsT_scale=w_s[:, a, rows],
+                        start=(a == 0),
+                        stop=(a == 1),
+                        **moving(a, c),
+                    )
+                ke.append(bank)
+            for c in range(CHUNKS):
+                bank = psum.tile([P, CHUNK], F32, name="ve")
+                nc.tensor.matmul_mx(
+                    out=bank[:],
+                    lhsT=wv8_w[:, rows].bitcast(FP8X4),
+                    lhsT_scale=wv8_s[:, rows],
+                    start=True,
+                    stop=False,
+                    **moving(0, c),
+                )
+                nc.tensor.matmul_mx(
+                    out=bank[:],
+                    lhsT=wv4_w[:, 2 * i * P : 2 * (i + 1) * P].bitcast(FP4X4),
+                    lhsT_scale=w_s[:, 2, rows],
+                    start=False,
+                    stop=True,
+                    **moving(1, c),
+                )
+                ve.append(bank)
+
+            gate = held.tile([P, J], F32, name="gate", tag=f"side{i % 2}")
+            for c in range(CHUNKS):
+                cols = slice(c * CHUNK, (c + 1) * CHUNK)
+                nc.vector.tensor_tensor(work[:, cols], ke[c][:], work[:, cols], MULT)
+                nc.scalar.activation(gate[:, cols], work[:, cols], SIGMOID)
+            for c in range(CHUNKS):
+                cols = slice(c * CHUNK, (c + 1) * CHUNK)
+                nc.vector.tensor_tensor(work[:, cols], ve[c][:], gate[:, cols], MULT)
+
+            listed = held.tile([P, J], F32, name="listed", tag=f"side{i % 2}")
+            if i < TILES - 1:
+                nc.vector.tensor_copy(listed[:], record[:].indirect(offsets[:]))
+                nc.gpsimd.tensor_tensor(work[:], work[:], listed[:], ADD)
+                nc.sync.dma_start(out=out[rows, :], in_=work[:])
+            else:
+                step = LIST_COLS // CHUNKS
+                for c in range(CHUNKS):
+                    cols = slice(c * CHUNK, (c + 1) * CHUNK)
+                    nc.vector.tensor_copy(listed[:, cols], record[:].indirect(offsets[:, c * step : (c + 1) * step]))
+                    nc.vector.tensor_tensor(work[:, cols], work[:, cols], listed[:, cols], ADD)
+                    nc.sync.dma_start(out=out[rows, cols], in_=work[:, cols])

@@ -27,6 +27,8 @@ TILES = N // P
 HALF = N // 2
 QUANT = 256
 LIST_COLS = J // 16
+LATE_QUANT_TILE = 2
+ALIGN = 64
 
 
 def tile_list_engram_qf_sigL_kernel(
@@ -35,49 +37,33 @@ def tile_list_engram_qf_sigL_kernel(
     nc = tc.nc
     with ExitStack() as ctx:
         held = ctx.enter_context(tc.tile_pool(name="held", bufs=1))
-        psum = ctx.enter_context(tc.psum_pool(name="psum", bufs=CHUNKS))
+        front = ctx.enter_context(tc.tile_pool(name="front", bufs=1))
+        psum = ctx.enter_context(tc.psum_pool(name="psum", bufs=1))
+
+        def tile(shape, dtype, tag):
+            return held.tile(shape, dtype, name=tag, tag=tag, align_bytes=ALIGN)
+
+        def placed(shape, dtype, tag, offset):
+            return front.tile(shape, dtype, name=tag, tag=tag, align_bytes=ALIGN, offset=offset)
 
         offsets = held.tile([P, LIST_COLS], U16, name="offsets")
         nc.sync.dma_start(offsets[:], offs)
 
-        tab_s = held.tile([P, T], U8, name="tab_s", tag="work4", align_bytes=64)
+        w_s = tile([P, 3, N], U8, "w_s")
+        nc.vector.memset(w_s[:].rearrange("p a n -> p (a n)").bitcast(I32), 0)
+
+        tab_s = placed([P, T], U8, "tab_s", 3072)
         nc.sync.dma_start(out=tab_s[0:32, :].bitcast(I32), in_=tab_scales.rearrange("a q t -> (a q) t").bitcast(I32))
         nc.vector.memset(tab_s[32:64, :].bitcast(I32), 0)
         nc.vector.memset(tab_s[64:128, :].bitcast(I32), 0)
-        tab_w = held.tile([P, T], U32, name="tab_w", tag="work1", align_bytes=64)
+        tab_w = tile([P, T], U32, "work1")
         nc.sync.dma_start(out=tab_w[:].bitcast(I32), in_=tab_words[0].rearrange("p t b -> p (t b)").bitcast(I32))
 
+        v_s = tile([P, 2, J], U8, "v_s")
+        nc.gpsimd.memset(v_s[:].rearrange("p a j -> p (a j)").bitcast(I32), 0)
         warm = held.tile([P, 8], F32, name="warm")
         nc.gpsimd.memset(warm[:], 0.0)
-        nc.scalar.activation(warm[:], warm[:], SIGMOID)
 
-        w_s = held.tile([P, 3, N], U8, name="w_s", align_bytes=64)
-        nc.gpsimd.memset(w_s[:].rearrange("p a n -> p (a n)").bitcast(I32), 0)
-        v_s = held.tile([P, 2, J], U8, name="v_s", align_bytes=64)
-        nc.gpsimd.memset(v_s[:].rearrange("p a j -> p (a j)").bitcast(I32), 0)
-
-        wv8_rows = wv8.rearrange("(p i) n -> p i n", i=PACK)
-        wk_rows = wk_words.rearrange("a p n b -> p a (n b)")
-
-        def load_wv8(h, tag):
-            raw = held.tile([P, PACK, HALF], F32, name="raw", tag=tag, align_bytes=64)
-            nc.sync.dma_start(out=raw[:], in_=wv8_rows[:, :, h * HALF : (h + 1) * HALF])
-            return raw
-
-        def load_wk(h, tag):
-            words = held.tile([P, 2, HALF], U32, name="words", tag=tag, align_bytes=64)
-            nc.sync.dma_start(
-                out=words[:].bitcast(I32), in_=wk_rows[:, :, 4 * h * HALF : 4 * (h + 1) * HALF].bitcast(I32)
-            )
-            return words
-
-        def load_st(i):
-            work = held.tile([P, J], F32, name="work", tag=f"work{i % 5}", align_bytes=64)
-            nc.sync.dma_start(out=work[:], in_=st[i * P : (i + 1) * P, :])
-            return work
-
-        wv8_raw = [load_wv8(0, "record0")]
-        wk_w = [load_wk(0, "wk0")]
         for q in range(QUADS):
             nc.scalar.dma_start(
                 out=w_s[32 * q : 32 * q + ROWS, 0:2, :].bitcast(I32),
@@ -88,10 +74,50 @@ def tile_list_engram_qf_sigL_kernel(
                 out=w_s[32 * q : 32 * q + ROWS, 2, :].bitcast(I32),
                 in_=wv4_scales[0, ROWS * q : ROWS * (q + 1), :].bitcast(I32),
             )
-        wv4_w = held.tile([P, 2 * N], U8, name="wv4_w", align_bytes=64)
-        nc.sync.dma_start(out=wv4_w[:].bitcast(I32), in_=wv4_words[0].bitcast(I32))
+        nc.scalar.activation(warm[:], warm[:], SIGMOID)
 
-        picked_s = held.tile([P, J], U8, name="picked_s", tag="wk1", align_bytes=64)
+        wv8_rows = wv8.rearrange("(p i) n -> p i n", i=PACK)
+        wk_rows = wk_words.rearrange("a p n b -> p a (n b)")
+
+        def load_wv8(h):
+            raw = tile([P, PACK, HALF], F32, "work3")
+            nc.sync.dma_start(out=raw[:], in_=wv8_rows[:, :, h * HALF : (h + 1) * HALF])
+            return raw
+
+        def load_wk(h, words):
+            nc.sync.dma_start(
+                out=words[:].bitcast(I32), in_=wk_rows[:, :, 4 * h * HALF : 4 * (h + 1) * HALF].bitcast(I32)
+            )
+            return words
+
+        def load_st(i):
+            if i % 5 == 0:
+                work = placed([P, J], F32, "work0", 6144)
+            else:
+                work = tile([P, J], F32, f"work{i % 5}")
+            nc.sync.dma_start(out=work[:], in_=st[i * P : (i + 1) * P, :])
+            return work
+
+        def load_record(i):
+            record = tile([P, T], F32, f"record{i % 3}")
+            nc.sync.dma_start(out=record[:], in_=rT[i * P : (i + 1) * P, :])
+            return record
+
+        def interleave(raw, grouped):
+            for c0 in range(0, HALF, QUANT):
+                nc.scalar.copy(grouped[:, c0 : c0 + QUANT, :], raw[:, :, c0 : c0 + QUANT].rearrange("p i n -> p n i"))
+
+        def quantize(grouped, codes, scales, c0, width):
+            nc.vector.quantize_mx(
+                out=codes[:, c0 : c0 + width].bitcast(FP8X4),
+                scales=scales[:, c0 : c0 + width],
+                in_=grouped[:, c0 : c0 + width, :].rearrange("p n i -> p (n i)"),
+            )
+
+        raw = load_wv8(0)
+        record = load_record(0)
+
+        picked_s = tile([P, J], U8, "wk1")
         nc.vector.tensor_copy(picked_s[:], tab_s[:].indirect(offsets[:]))
         for a in range(2):
             for q in range(QUADS):
@@ -100,11 +126,14 @@ def tile_list_engram_qf_sigL_kernel(
                     out=v_s[32 * q : 32 * q + ROWS, a, :].bitcast(I32),
                     in_=picked_s[row : row + ROWS, :].bitcast(I32),
                 )
-        wv8_raw.append(load_wv8(1, "work4"))
-        v_w = held.tile([P, 2, 2 * J], U8, name="v_w", align_bytes=64)
+        wk_w = [load_wk(0, placed([P, 2, HALF], U32, "wk0", 0))]
+        wv4_w = placed([P, 2 * N], U8, "wv4_w", 4096)
+        nc.sync.dma_start(out=wv4_w[:].bitcast(I32), in_=wv4_words[0].bitcast(I32))
+
+        v_w = tile([P, 2, 2 * J], U8, "v_w")
         picked_w = []
         for h, tag in enumerate(("record1", "work2")):
-            picked = held.tile([P, J // 2], U32, name="picked", tag=tag, align_bytes=64)
+            picked = tile([P, J // 2], U32, tag)
             nc.vector.tensor_copy(
                 picked[:], tab_w[:].indirect(offsets[:, h * LIST_COLS // 2 : (h + 1) * LIST_COLS // 2])
             )
@@ -114,22 +143,17 @@ def tile_list_engram_qf_sigL_kernel(
                 v_w[:].bitcast(U16)[:, :, h * J // 2 : (h + 1) * J // 2],
                 picked_w[h][:].bitcast(U16).rearrange("p (j d) -> p d j", d=2),
             )
-        wk_w.append(load_wk(1, "wk1"))
+        wk_w.append(load_wk(1, tile([P, 2, HALF], U32, "wk1")))
 
-        wv8_w = held.tile([P, N], U32, name="wv8_w", align_bytes=64)
-        wv8_s = held.tile([P, N], U8, name="wv8_s", align_bytes=64)
-        for h, tag in enumerate(("record2", "work3")):
-            grouped = held.tile([P, HALF, PACK], BF16, name="grouped", tag=tag, align_bytes=64)
-            for c0 in range(0, HALF, QUANT):
-                n0 = h * HALF + c0
-                nc.scalar.copy(
-                    grouped[:, c0 : c0 + QUANT, :], wv8_raw[h][:, :, c0 : c0 + QUANT].rearrange("p i n -> p n i")
-                )
-                nc.vector.quantize_mx(
-                    out=wv8_w[:, n0 : n0 + QUANT].bitcast(FP8X4),
-                    scales=wv8_s[:, n0 : n0 + QUANT],
-                    in_=grouped[:, c0 : c0 + QUANT, :].rearrange("p n i -> p (n i)"),
-                )
+        wv8_s = [tile([P, HALF], U8, f"wv8_s{h}") for h in range(2)]
+        wv8_w = [tile([P, HALF], U32, "wv8_w0")]
+        grouped = tile([P, HALF, PACK], BF16, "record2")
+        interleave(raw, grouped)
+        for c0 in range(0, HALF, QUANT):
+            quantize(grouped, wv8_w[0], wv8_s[0], c0, QUANT)
+        raw = load_wv8(1)
+        grouped = tile([P, HALF, PACK], BF16, "work4")
+        interleave(raw, grouped)
 
         def moving(a, c):
             return dict(
@@ -137,32 +161,23 @@ def tile_list_engram_qf_sigL_kernel(
                 rhs_scale=v_s[:, a, c * CHUNK : (c + 1) * CHUNK],
             )
 
+        listed = tile([P, J], F32, "side0")
+        nc.vector.tensor_copy(listed[:], record[:].indirect(offsets[:]))
+
         for i in range(TILES):
             rows = slice(i * P, (i + 1) * P)
             work = load_st(i)
-            record = held.tile([P, T], F32, name="record", tag=f"record{i % 3}", align_bytes=64)
-            nc.sync.dma_start(out=record[:], in_=rT[rows, :])
+            if i > 0:
+                record = load_record(i)
 
-            c0 = (i * P) % HALF
+            h, c0 = divmod(i * P, HALF)
             ke, ve = [], []
             for c in range(CHUNKS):
-                bank = psum.tile([P, CHUNK], F32, name="ke")
-                for a in range(2):
-                    nc.tensor.matmul_mx(
-                        out=bank[:],
-                        lhsT=wk_w[i * P // HALF][:, a, c0 : c0 + P].bitcast(FP8X4),
-                        lhsT_scale=w_s[:, a, rows],
-                        start=(a == 0),
-                        stop=(a == 1),
-                        **moving(a, c),
-                    )
-                ke.append(bank)
-            for c in range(CHUNKS):
-                bank = psum.tile([P, CHUNK], F32, name="ve")
+                bank = psum.tile([P, CHUNK], F32, name=f"bank{c + CHUNKS * (i % 2)}")
                 nc.tensor.matmul_mx(
                     out=bank[:],
-                    lhsT=wv8_w[:, rows].bitcast(FP8X4),
-                    lhsT_scale=wv8_s[:, rows],
+                    lhsT=wv8_w[h][:, c0 : c0 + P].bitcast(FP8X4),
+                    lhsT_scale=wv8_s[h][:, c0 : c0 + P],
                     start=True,
                     stop=False,
                     **moving(0, c),
@@ -176,25 +191,51 @@ def tile_list_engram_qf_sigL_kernel(
                     **moving(1, c),
                 )
                 ve.append(bank)
+            for c in range(CHUNKS):
+                bank = psum.tile([P, CHUNK], F32, name=f"bank{c + CHUNKS * ((i + 1) % 2)}")
+                for a in range(2):
+                    nc.tensor.matmul_mx(
+                        out=bank[:],
+                        lhsT=wk_w[h][:, a, c0 : c0 + P].bitcast(FP8X4),
+                        lhsT_scale=w_s[:, a, rows],
+                        start=(a == 0),
+                        stop=(a == 1),
+                        **moving(a, c),
+                    )
+                ke.append(bank)
 
-            gate = held.tile([P, J], F32, name="gate", tag=f"side{i % 2}")
+            gate_lo = tile([P, 2, CHUNK], F32, f"side{max(i, 1) % 2}")
+            gate_2 = tile([P, CHUNK], F32, "wv8_w1" if i == LATE_QUANT_TILE else "gate2")
+            gate_3 = tile([P, CHUNK], F32, "gate3")
+            gate = [gate_lo[:, 0, :], gate_lo[:, 1, :], gate_2[:], gate_3[:]]
             for c in range(CHUNKS):
                 cols = slice(c * CHUNK, (c + 1) * CHUNK)
                 nc.vector.tensor_tensor(work[:, cols], ke[c][:], work[:, cols], MULT)
-                nc.scalar.activation(gate[:, cols], work[:, cols], SIGMOID)
+                nc.scalar.activation(gate[c], work[:, cols], SIGMOID)
             for c in range(CHUNKS):
                 cols = slice(c * CHUNK, (c + 1) * CHUNK)
-                nc.vector.tensor_tensor(work[:, cols], ve[c][:], gate[:, cols], MULT)
+                nc.vector.tensor_tensor(work[:, cols], ve[c][:], gate[c], MULT)
 
-            listed = held.tile([P, J], F32, name="listed", tag=f"side{i % 2}")
+            if i == LATE_QUANT_TILE:
+                wv8_w.append(tile([P, HALF], U32, "wv8_w1"))
+                quantize(grouped, wv8_w[1], wv8_s[1], 0, HALF)
+
+            if i > 0:
+                listed = tile([P, J], F32, f"side{i % 2}")
             if i < TILES - 1:
-                nc.vector.tensor_copy(listed[:], record[:].indirect(offsets[:]))
+                if i > 0:
+                    nc.vector.tensor_copy(listed[:], record[:].indirect(offsets[:]))
                 nc.gpsimd.tensor_tensor(work[:], work[:], listed[:], ADD)
                 nc.sync.dma_start(out=out[rows, :], in_=work[:])
             else:
                 step = LIST_COLS // CHUNKS
-                for c in range(CHUNKS):
-                    cols = slice(c * CHUNK, (c + 1) * CHUNK)
-                    nc.vector.tensor_copy(listed[:, cols], record[:].indirect(offsets[:, c * step : (c + 1) * step]))
-                    nc.vector.tensor_tensor(work[:, cols], work[:, cols], listed[:, cols], ADD)
-                    nc.sync.dma_start(out=out[rows, cols], in_=work[:, cols])
+                for c in range(CHUNKS + 1):
+                    if c < CHUNKS:
+                        nc.vector.tensor_copy(
+                            listed[:, c * CHUNK : (c + 1) * CHUNK],
+                            record[:].indirect(offsets[:, c * step : (c + 1) * step]),
+                        )
+                    if c > 0:
+                        cols = slice((c - 1) * CHUNK, c * CHUNK)
+                        nc.vector.tensor_tensor(work[:, cols], work[:, cols], listed[:, cols], ADD)
+                        nc.sync.dma_start(out=out[rows, cols], in_=work[:, cols])

@@ -27,7 +27,8 @@ TILES = N // P
 HALF = N // 2
 QUANT = 256
 LIST_COLS = J // 16
-LATE_QUANT_TILE = 2
+SHARED = 2
+KIB = 1024
 ALIGN = 64
 
 
@@ -60,29 +61,23 @@ def tile_list_engram_qf_sigL_kernel(
         nc.sync.dma_start(out=tab_w[:].bitcast(I32), in_=tab_words[0].rearrange("p t b -> p (t b)").bitcast(I32))
 
         v_s = tile([P, 2, J], U8, "v_s")
-        nc.gpsimd.memset(v_s[:].rearrange("p a j -> p (a j)").bitcast(I32), 0)
+        nc.vector.memset(v_s[:].rearrange("p a j -> p (a j)").bitcast(I32), 0)
         warm = held.tile([P, 8], F32, name="warm")
         nc.gpsimd.memset(warm[:], 0.0)
 
         for q in range(QUADS):
-            nc.scalar.dma_start(
+            nc.gpsimd.dma_start(
                 out=w_s[32 * q : 32 * q + ROWS, 0:2, :].bitcast(I32),
                 in_=wk_scales[:, ROWS * q : ROWS * (q + 1), :].rearrange("a r n -> r a n").bitcast(I32),
             )
         for q in range(QUADS):
-            nc.scalar.dma_start(
+            nc.gpsimd.dma_start(
                 out=w_s[32 * q : 32 * q + ROWS, 2, :].bitcast(I32),
                 in_=wv4_scales[0, ROWS * q : ROWS * (q + 1), :].bitcast(I32),
             )
         nc.scalar.activation(warm[:], warm[:], SIGMOID)
 
-        wv8_rows = wv8.rearrange("(p i) n -> p i n", i=PACK)
         wk_rows = wk_words.rearrange("a p n b -> p a (n b)")
-
-        def load_wv8(h):
-            raw = tile([P, PACK, HALF], F32, "work3")
-            nc.sync.dma_start(out=raw[:], in_=wv8_rows[:, :, h * HALF : (h + 1) * HALF])
-            return raw
 
         def load_wk(h, words):
             nc.sync.dma_start(
@@ -90,31 +85,27 @@ def tile_list_engram_qf_sigL_kernel(
             )
             return words
 
+        work_at = {0: 6 * KIB, 3: 30 * KIB, 4: 54 * KIB}
+        record_at = {0: 58 * KIB, 2: 14 * KIB, 3: 38 * KIB, 4: 62 * KIB, 7: 14 * KIB}
+
         def load_st(i):
-            if i % 5 == 0:
-                work = placed([P, J], F32, "work0", 6144)
+            if i in work_at:
+                work = placed([P, J], F32, f"work{i}", work_at[i])
             else:
-                work = tile([P, J], F32, f"work{i % 5}")
+                work = tile([P, J], F32, f"work{i}")
             nc.sync.dma_start(out=work[:], in_=st[i * P : (i + 1) * P, :])
             return work
 
         def load_record(i):
-            record = tile([P, T], F32, f"record{i % 3}")
+            if i in record_at:
+                record = placed([P, T], F32, f"record{i}", record_at[i])
+            else:
+                record = tile([P, T], F32, "record5" if i == 5 else "record1")
             nc.sync.dma_start(out=record[:], in_=rT[i * P : (i + 1) * P, :])
             return record
 
-        def interleave(raw, grouped):
-            for c0 in range(0, HALF, QUANT):
-                nc.scalar.copy(grouped[:, c0 : c0 + QUANT, :], raw[:, :, c0 : c0 + QUANT].rearrange("p i n -> p n i"))
-
-        def quantize(grouped, codes, scales, c0, width):
-            nc.vector.quantize_mx(
-                out=codes[:, c0 : c0 + width].bitcast(FP8X4),
-                scales=scales[:, c0 : c0 + width],
-                in_=grouped[:, c0 : c0 + width, :].rearrange("p n i -> p (n i)"),
-            )
-
-        raw = load_wv8(0)
+        raw = placed([P, PACK, N], F32, "raw", 26 * KIB)
+        nc.sync.dma_start(out=raw[:], in_=wv8.rearrange("(p i) n -> p i n", i=PACK))
         record = load_record(0)
 
         picked_s = tile([P, J], U8, "wk1")
@@ -145,15 +136,17 @@ def tile_list_engram_qf_sigL_kernel(
             )
         wk_w.append(load_wk(1, tile([P, 2, HALF], U32, "wk1")))
 
-        wv8_s = [tile([P, HALF], U8, f"wv8_s{h}") for h in range(2)]
-        wv8_w = [tile([P, HALF], U32, "wv8_w0")]
-        grouped = tile([P, HALF, PACK], BF16, "record2")
-        interleave(raw, grouped)
-        for c0 in range(0, HALF, QUANT):
-            quantize(grouped, wv8_w[0], wv8_s[0], c0, QUANT)
-        raw = load_wv8(1)
-        grouped = tile([P, HALF, PACK], BF16, "work4")
-        interleave(raw, grouped)
+        wv8_s = tile([P, N], U8, "wv8_s")
+        wv8_w = tile([P, N], U32, "wv8_w")
+        grouped = tile([P, N, PACK], BF16, "record5")
+        for n0 in range(0, N, QUANT):
+            cols = slice(n0, n0 + QUANT)
+            nc.scalar.copy(grouped[:, cols, :], raw[:, :, cols].rearrange("p i n -> p n i"))
+            nc.vector.quantize_mx(
+                out=wv8_w[:, cols].bitcast(FP8X4),
+                scales=wv8_s[:, cols],
+                in_=grouped[:, cols, :].rearrange("p n i -> p (n i)"),
+            )
 
         def moving(a, c):
             return dict(
@@ -161,9 +154,10 @@ def tile_list_engram_qf_sigL_kernel(
                 rhs_scale=v_s[:, a, c * CHUNK : (c + 1) * CHUNK],
             )
 
-        listed = tile([P, J], F32, "side0")
+        listed = tile([P, J], F32, "listed0")
         nc.vector.tensor_copy(listed[:], record[:].indirect(offsets[:]))
 
+        stores = []
         for i in range(TILES):
             rows = slice(i * P, (i + 1) * P)
             work = load_st(i)
@@ -176,8 +170,8 @@ def tile_list_engram_qf_sigL_kernel(
                 bank = psum.tile([P, CHUNK], F32, name=f"bank{c + CHUNKS * (i % 2)}")
                 nc.tensor.matmul_mx(
                     out=bank[:],
-                    lhsT=wv8_w[h][:, c0 : c0 + P].bitcast(FP8X4),
-                    lhsT_scale=wv8_s[h][:, c0 : c0 + P],
+                    lhsT=wv8_w[:, rows].bitcast(FP8X4),
+                    lhsT_scale=wv8_s[:, rows],
                     start=True,
                     stop=False,
                     **moving(0, c),
@@ -204,38 +198,45 @@ def tile_list_engram_qf_sigL_kernel(
                     )
                 ke.append(bank)
 
-            gate_lo = tile([P, 2, CHUNK], F32, f"side{max(i, 1) % 2}")
-            gate_2 = tile([P, CHUNK], F32, "wv8_w1" if i == LATE_QUANT_TILE else "gate2")
-            gate_3 = tile([P, CHUNK], F32, "gate3")
+            last = i == TILES - 1
+            shared = 0 if last else SHARED
+            gate_lo = tile([P, 2, CHUNK], F32, f"gate_lo{i % 2}")
+            gate_2 = tile([P, CHUNK], F32, "gate2")
+            gate_3 = tile([P, CHUNK], F32, f"work{i + 5}" if i + 5 < TILES else "gate3")
             gate = [gate_lo[:, 0, :], gate_lo[:, 1, :], gate_2[:], gate_3[:]]
+            if shared:
+                value = tile([P, SHARED, CHUNK], F32, f"value{i % 2}")
+                for c in range(SHARED):
+                    nc.scalar.copy(value[:, c, :], ve[c][:])
             for c in range(CHUNKS):
                 cols = slice(c * CHUNK, (c + 1) * CHUNK)
                 nc.vector.tensor_tensor(work[:, cols], ke[c][:], work[:, cols], MULT)
                 nc.scalar.activation(gate[c], work[:, cols], SIGMOID)
-            for c in range(CHUNKS):
+            if shared:
+                nc.gpsimd.tensor_tensor(
+                    work[:, 0 : SHARED * CHUNK],
+                    value[:].rearrange("p c j -> p (c j)"),
+                    gate_lo[:].rearrange("p c j -> p (c j)"),
+                    MULT,
+                )
+            for c in range(shared, CHUNKS):
                 cols = slice(c * CHUNK, (c + 1) * CHUNK)
                 nc.vector.tensor_tensor(work[:, cols], ve[c][:], gate[c], MULT)
 
-            if i == LATE_QUANT_TILE:
-                wv8_w.append(tile([P, HALF], U32, "wv8_w1"))
-                quantize(grouped, wv8_w[1], wv8_s[1], 0, HALF)
-
             if i > 0:
-                listed = tile([P, J], F32, f"side{i % 2}")
-            if i < TILES - 1:
+                listed = tile([P, J], F32, f"listed{i % 2}")
+            if not last:
                 if i > 0:
                     nc.vector.tensor_copy(listed[:], record[:].indirect(offsets[:]))
                 nc.gpsimd.tensor_tensor(work[:], work[:], listed[:], ADD)
-                nc.sync.dma_start(out=out[rows, :], in_=work[:])
+                stores.append((out[rows, :], work[:]))
             else:
+                for dst, src in stores:
+                    nc.sync.dma_start(out=dst, in_=src)
                 step = LIST_COLS // CHUNKS
-                for c in range(CHUNKS + 1):
-                    if c < CHUNKS:
-                        nc.vector.tensor_copy(
-                            listed[:, c * CHUNK : (c + 1) * CHUNK],
-                            record[:].indirect(offsets[:, c * step : (c + 1) * step]),
-                        )
-                    if c > 0:
-                        cols = slice((c - 1) * CHUNK, c * CHUNK)
-                        nc.vector.tensor_tensor(work[:, cols], work[:, cols], listed[:, cols], ADD)
-                        nc.sync.dma_start(out=out[rows, cols], in_=work[:, cols])
+                for c in range(CHUNKS):
+                    cols = slice(c * CHUNK, (c + 1) * CHUNK)
+                    nc.vector.tensor_copy(listed[:, cols], record[:].indirect(offsets[:, c * step : (c + 1) * step]))
+                    adder = nc.vector if c == CHUNKS - 1 else nc.gpsimd
+                    adder.tensor_tensor(work[:, cols], work[:, cols], listed[:, cols], ADD)
+                    nc.sync.dma_start(out=out[rows, cols], in_=work[:, cols])

@@ -27,7 +27,7 @@ TILES = N // P
 HALF = N // 2
 QUANT = 256
 LIST_COLS = J // 16
-SHARED = 2
+SHARED = (2, 2, 2, 3, 3, 3, 3, 0)
 KIB = 1024
 ALIGN = 64
 
@@ -199,29 +199,29 @@ def tile_list_engram_qf_sigL_kernel(
                 ke.append(bank)
 
             last = i == TILES - 1
-            shared = 0 if last else SHARED
-            gate_lo = tile([P, 2, CHUNK], F32, f"gate_lo{i % 2}")
-            gate_2 = tile([P, CHUNK], F32, "gate2")
-            gate_3 = tile([P, CHUNK], F32, f"work{i + 5}" if i + 5 < TILES else "gate3")
-            gate = [gate_lo[:, 0, :], gate_lo[:, 1, :], gate_2[:], gate_3[:]]
+            shared = SHARED[i]
+            own = CHUNKS - shared
+            gate_0 = tile([P, CHUNK], F32, f"listed{max(i, 1) % 2}")
+            gate_rest = tile([P, CHUNKS - 1, CHUNK], F32, f"gate{i % 2}")
+            gate = [gate_0[:]] + [gate_rest[:, c, :] for c in range(CHUNKS - 1)]
             if shared:
-                value = tile([P, SHARED, CHUNK], F32, f"value{i % 2}")
-                for c in range(SHARED):
-                    nc.scalar.copy(value[:, c, :], ve[c][:])
+                value = tile([P, shared, CHUNK], F32, f"work{i + 5}" if i + 5 < TILES else f"value{i % 2}")
+                for c in range(own, CHUNKS):
+                    nc.scalar.copy(value[:, c - own, :], ve[c][:])
             for c in range(CHUNKS):
                 cols = slice(c * CHUNK, (c + 1) * CHUNK)
                 nc.vector.tensor_tensor(work[:, cols], ke[c][:], work[:, cols], MULT)
                 nc.scalar.activation(gate[c], work[:, cols], SIGMOID)
-            if shared:
-                nc.gpsimd.tensor_tensor(
-                    work[:, 0 : SHARED * CHUNK],
-                    value[:].rearrange("p c j -> p (c j)"),
-                    gate_lo[:].rearrange("p c j -> p (c j)"),
-                    MULT,
-                )
-            for c in range(shared, CHUNKS):
+            for c in range(own):
                 cols = slice(c * CHUNK, (c + 1) * CHUNK)
                 nc.vector.tensor_tensor(work[:, cols], ve[c][:], gate[c], MULT)
+            if shared:
+                nc.gpsimd.tensor_tensor(
+                    work[:, own * CHUNK :],
+                    value[:].rearrange("p c j -> p (c j)"),
+                    gate_rest[:, own - 1 :, :].rearrange("p c j -> p (c j)"),
+                    MULT,
+                )
 
             if i > 0:
                 listed = tile([P, J], F32, f"listed{i % 2}")

@@ -19,7 +19,6 @@ SIGMOID = mybir.ActivationFunctionType.Sigmoid
 
 P = 128
 PACK = 4
-QUADS = 4
 ROWS = 4
 CHUNK = 512
 CHUNKS = J // CHUNK
@@ -27,7 +26,7 @@ TILES = N // P
 HALF = N // 2
 QUANT = 256
 LIST_COLS = J // 16
-SHARED = (2, 2, 2, 3, 3, 3, 3, 0)
+SHARED = (0, 3, 2, 3, 3, 3, 3, 0)
 KIB = 1024
 ALIGN = 64
 
@@ -62,20 +61,14 @@ def tile_list_engram_qf_sigL_kernel(
 
         v_s = tile([P, 2, J], U8, "v_s")
         nc.vector.memset(v_s[:].rearrange("p a j -> p (a j)").bitcast(I32), 0)
-        warm = held.tile([P, 8], F32, name="warm")
-        nc.gpsimd.memset(warm[:], 0.0)
 
-        for q in range(QUADS):
+        for r in range(ROWS):
             nc.gpsimd.dma_start(
-                out=w_s[32 * q : 32 * q + ROWS, 0:2, :].bitcast(I32),
-                in_=wk_scales[:, ROWS * q : ROWS * (q + 1), :].rearrange("a r n -> r a n").bitcast(I32),
+                out=w_s[r:P:32, 0:2, :].bitcast(I32),
+                in_=wk_scales[:, r:16:ROWS, :].rearrange("a q n -> q a n").bitcast(I32),
             )
-        for q in range(QUADS):
-            nc.gpsimd.dma_start(
-                out=w_s[32 * q : 32 * q + ROWS, 2, :].bitcast(I32),
-                in_=wv4_scales[0, ROWS * q : ROWS * (q + 1), :].bitcast(I32),
-            )
-        nc.scalar.activation(warm[:], warm[:], SIGMOID)
+        for r in range(ROWS):
+            nc.gpsimd.dma_start(out=w_s[r:P:32, 2, :].bitcast(I32), in_=wv4_scales[0, r:16:ROWS, :].bitcast(I32))
 
         wk_rows = wk_words.rearrange("a p n b -> p a (n b)")
 
@@ -111,11 +104,10 @@ def tile_list_engram_qf_sigL_kernel(
         picked_s = tile([P, J], U8, "wk1")
         nc.vector.tensor_copy(picked_s[:], tab_s[:].indirect(offsets[:]))
         for a in range(2):
-            for q in range(QUADS):
-                row = 16 * a + ROWS * q
+            for r in range(ROWS):
                 nc.scalar.dma_start(
-                    out=v_s[32 * q : 32 * q + ROWS, a, :].bitcast(I32),
-                    in_=picked_s[row : row + ROWS, :].bitcast(I32),
+                    out=v_s[r:P:32, a, :].bitcast(I32),
+                    in_=picked_s[16 * a + r : 16 * (a + 1) : ROWS, :].bitcast(I32),
                 )
         wk_w = [load_wk(0, placed([P, 2, HALF], U32, "wk0", 0))]
         wv4_w = placed([P, 2 * N], U8, "wv4_w", 4096)
@@ -202,10 +194,10 @@ def tile_list_engram_qf_sigL_kernel(
             shared = SHARED[i]
             own = CHUNKS - shared
             gate_0 = tile([P, CHUNK], F32, f"listed{max(i, 1) % 2}")
-            gate_rest = tile([P, CHUNKS - 1, CHUNK], F32, f"gate{i % 2}")
+            gate_rest = tile([P, CHUNKS - 1, CHUNK], F32, f"work{i + 5}" if i + 5 < TILES else f"gate{i % 2}")
             gate = [gate_0[:]] + [gate_rest[:, c, :] for c in range(CHUNKS - 1)]
             if shared:
-                value = tile([P, shared, CHUNK], F32, f"work{i + 5}" if i + 5 < TILES else f"value{i % 2}")
+                value = tile([P, shared, CHUNK], F32, f"value{i % 2}")
                 for c in range(own, CHUNKS):
                     nc.scalar.copy(value[:, c - own, :], ve[c][:])
             for c in range(CHUNKS):

@@ -26,7 +26,7 @@ TILES = N // P
 HALF = N // 2
 QUANT = 256
 LIST_COLS = J // 16
-SHARED = (0, 3, 2, 3, 3, 3, 3, 0)
+OWN = (0, 1, 1, 1, 1, 1, 2, 4)
 KIB = 1024
 ALIGN = 64
 
@@ -52,11 +52,11 @@ def tile_list_engram_qf_sigL_kernel(
         w_s = tile([P, 3, N], U8, "w_s")
         nc.vector.memset(w_s[:].rearrange("p a n -> p (a n)").bitcast(I32), 0)
 
-        tab_s = placed([P, T], U8, "tab_s", 3072)
+        tab_s = placed([P, T], U8, "tab_s", 140 * KIB)
         nc.sync.dma_start(out=tab_s[0:32, :].bitcast(I32), in_=tab_scales.rearrange("a q t -> (a q) t").bitcast(I32))
         nc.vector.memset(tab_s[32:64, :].bitcast(I32), 0)
         nc.vector.memset(tab_s[64:128, :].bitcast(I32), 0)
-        tab_w = tile([P, T], U32, "work1")
+        tab_w = placed([P, T], U32, "tab_w", 14 * KIB)
         nc.sync.dma_start(out=tab_w[:].bitcast(I32), in_=tab_words[0].rearrange("p t b -> p (t b)").bitcast(I32))
 
         v_s = tile([P, 2, J], U8, "v_s")
@@ -68,7 +68,7 @@ def tile_list_engram_qf_sigL_kernel(
                 in_=wk_scales[:, r:16:ROWS, :].rearrange("a q n -> q a n").bitcast(I32),
             )
         for r in range(ROWS):
-            nc.gpsimd.dma_start(out=w_s[r:P:32, 2, :].bitcast(I32), in_=wv4_scales[0, r:16:ROWS, :].bitcast(I32))
+            nc.scalar.dma_start(out=w_s[r:P:32, 2, :].bitcast(I32), in_=wv4_scales[0, r:16:ROWS, :].bitcast(I32))
 
         wk_rows = wk_words.rearrange("a p n b -> p a (n b)")
 
@@ -78,30 +78,26 @@ def tile_list_engram_qf_sigL_kernel(
             )
             return words
 
-        work_at = {0: 6 * KIB, 3: 30 * KIB, 4: 54 * KIB}
-        record_at = {0: 58 * KIB, 2: 14 * KIB, 3: 38 * KIB, 4: 62 * KIB, 7: 14 * KIB}
+        state_at = [k * KIB for k in (140, 16, 44, 68, 92, 116, 0, 8)]
+        record_at = [k * KIB for k in (0, 28, 52, 76, 100, 124, 28, 52)]
 
         def load_st(i):
-            if i in work_at:
-                work = placed([P, J], F32, f"work{i}", work_at[i])
-            else:
-                work = tile([P, J], F32, f"work{i}")
-            nc.sync.dma_start(out=work[:], in_=st[i * P : (i + 1) * P, :])
-            return work
+            state = placed([P, J], F32, f"state{i}", state_at[i])
+            nc.sync.dma_start(out=state[:], in_=st[i * P : (i + 1) * P, :])
+            return state[:]
 
         def load_record(i):
-            if i in record_at:
-                record = placed([P, T], F32, f"record{i}", record_at[i])
-            else:
-                record = tile([P, T], F32, "record5" if i == 5 else "record1")
+            record = placed([P, T], F32, f"record{i}", record_at[i])
             nc.sync.dma_start(out=record[:], in_=rT[i * P : (i + 1) * P, :])
             return record
 
-        raw = placed([P, PACK, N], F32, "raw", 26 * KIB)
+        raw = placed([P, PACK, N], F32, "raw", 124 * KIB)
         nc.sync.dma_start(out=raw[:], in_=wv8.rearrange("(p i) n -> p i n", i=PACK))
-        record = load_record(0)
+        wk_w = [load_wk(0, tile([P, 2, HALF], U32, "wk0"))]
+        wv4_w = tile([P, 2 * N], U8, "wv4_w")
+        nc.sync.dma_start(out=wv4_w[:].bitcast(I32), in_=wv4_words[0].bitcast(I32))
 
-        picked_s = tile([P, J], U8, "wk1")
+        picked_s = placed([P, J], U8, "picked_s", 156 * KIB)
         nc.vector.tensor_copy(picked_s[:], tab_s[:].indirect(offsets[:]))
         for a in range(2):
             for r in range(ROWS):
@@ -109,28 +105,12 @@ def tile_list_engram_qf_sigL_kernel(
                     out=v_s[r:P:32, a, :].bitcast(I32),
                     in_=picked_s[16 * a + r : 16 * (a + 1) : ROWS, :].bitcast(I32),
                 )
-        wk_w = [load_wk(0, placed([P, 2, HALF], U32, "wk0", 0))]
-        wv4_w = placed([P, 2 * N], U8, "wv4_w", 4096)
-        nc.sync.dma_start(out=wv4_w[:].bitcast(I32), in_=wv4_words[0].bitcast(I32))
-
-        v_w = tile([P, 2, 2 * J], U8, "v_w")
-        picked_w = []
-        for h, tag in enumerate(("record1", "work2")):
-            picked = tile([P, J // 2], U32, tag)
-            nc.vector.tensor_copy(
-                picked[:], tab_w[:].indirect(offsets[:, h * LIST_COLS // 2 : (h + 1) * LIST_COLS // 2])
-            )
-            picked_w.append(picked)
-        for h in range(2):
-            nc.vector.tensor_copy(
-                v_w[:].bitcast(U16)[:, :, h * J // 2 : (h + 1) * J // 2],
-                picked_w[h][:].bitcast(U16).rearrange("p (j d) -> p d j", d=2),
-            )
-        wk_w.append(load_wk(1, tile([P, 2, HALF], U32, "wk1")))
+        state = load_st(0)
 
         wv8_s = tile([P, N], U8, "wv8_s")
         wv8_w = tile([P, N], U32, "wv8_w")
-        grouped = tile([P, N, PACK], BF16, "record5")
+
+        grouped = placed([P, N, PACK], BF16, "grouped", 148 * KIB)
         for n0 in range(0, N, QUANT):
             cols = slice(n0, n0 + QUANT)
             nc.scalar.copy(grouped[:, cols, :], raw[:, :, cols].rearrange("p i n -> p n i"))
@@ -140,95 +120,110 @@ def tile_list_engram_qf_sigL_kernel(
                 in_=grouped[:, cols, :].rearrange("p n i -> p (n i)"),
             )
 
+        v_w = tile([P, 2, 2 * J], U8, "v_w")
+        step = LIST_COLS // CHUNKS
+        picked_w = []
+        for c in range(CHUNKS):
+            picked = placed([P, CHUNK], U32, f"picked{c}", record_at[c + 2] - KIB if c < CHUNKS - 1 else state_at[5])
+            nc.vector.tensor_copy(picked[:], tab_w[:].indirect(offsets[:, c * step : (c + 1) * step]))
+            picked_w.append(picked)
+        for c in range(CHUNKS):
+            nc.vector.tensor_copy(
+                v_w[:].bitcast(U16)[:, :, c * CHUNK : (c + 1) * CHUNK],
+                picked_w[c][:].bitcast(U16).rearrange("p (j d) -> p d j", d=2),
+            )
+
         def moving(a, c):
             return dict(
                 rhs=v_w[:, a, 2 * c * CHUNK : 2 * (c + 1) * CHUNK].bitcast(FP4X4),
                 rhs_scale=v_s[:, a, c * CHUNK : (c + 1) * CHUNK],
             )
 
-        listed = tile([P, J], F32, "listed0")
-        nc.vector.tensor_copy(listed[:], record[:].indirect(offsets[:]))
+        def value_sum(i, c):
+            rows = slice(i * P, (i + 1) * P)
+            bank = psum.tile([P, CHUNK], F32, name=f"bank{c + CHUNKS * (i % 2)}")
+            nc.tensor.matmul_mx(
+                out=bank[:],
+                lhsT=wv8_w[:, rows].bitcast(FP8X4),
+                lhsT_scale=wv8_s[:, rows],
+                start=True,
+                stop=False,
+                **moving(0, c),
+            )
+            nc.tensor.matmul_mx(
+                out=bank[:],
+                lhsT=wv4_w[:, 2 * i * P : 2 * (i + 1) * P].bitcast(FP4X4),
+                lhsT_scale=w_s[:, 2, rows],
+                start=False,
+                stop=True,
+                **moving(1, c),
+            )
+            return bank
+
+        def key_sum(i, c):
+            h, c0 = divmod(i * P, HALF)
+            bank = psum.tile([P, CHUNK], F32, name=f"bank{c + CHUNKS * ((i + 1) % 2)}")
+            for a in range(2):
+                nc.tensor.matmul_mx(
+                    out=bank[:],
+                    lhsT=wk_w[h][:, a, c0 : c0 + P].bitcast(FP8X4),
+                    lhsT_scale=w_s[:, a, i * P : (i + 1) * P],
+                    start=(a == 0),
+                    stop=(a == 1),
+                    **moving(a, c),
+                )
+            return bank
 
         stores = []
         for i in range(TILES):
             rows = slice(i * P, (i + 1) * P)
-            work = load_st(i)
             if i > 0:
-                record = load_record(i)
+                state = load_st(i)
+            record = load_record(i)
+            if i == 3:
+                wk_w.append(load_wk(1, placed([P, 2, HALF], U32, "wk1", 24 * KIB)))
 
-            h, c0 = divmod(i * P, HALF)
-            ke, ve = [], []
-            for c in range(CHUNKS):
-                bank = psum.tile([P, CHUNK], F32, name=f"bank{c + CHUNKS * (i % 2)}")
-                nc.tensor.matmul_mx(
-                    out=bank[:],
-                    lhsT=wv8_w[:, rows].bitcast(FP8X4),
-                    lhsT_scale=wv8_s[:, rows],
-                    start=True,
-                    stop=False,
-                    **moving(0, c),
-                )
-                nc.tensor.matmul_mx(
-                    out=bank[:],
-                    lhsT=wv4_w[:, 2 * i * P : 2 * (i + 1) * P].bitcast(FP4X4),
-                    lhsT_scale=w_s[:, 2, rows],
-                    start=False,
-                    stop=True,
-                    **moving(1, c),
-                )
-                ve.append(bank)
-            for c in range(CHUNKS):
-                bank = psum.tile([P, CHUNK], F32, name=f"bank{c + CHUNKS * ((i + 1) % 2)}")
-                for a in range(2):
-                    nc.tensor.matmul_mx(
-                        out=bank[:],
-                        lhsT=wk_w[h][:, a, c0 : c0 + P].bitcast(FP8X4),
-                        lhsT_scale=w_s[:, a, rows],
-                        start=(a == 0),
-                        stop=(a == 1),
-                        **moving(a, c),
-                    )
-                ke.append(bank)
+            if i == 0:
+                ke = [key_sum(i, c) for c in range(CHUNKS)]
+                ve = [value_sum(i, c) for c in range(CHUNKS)]
+            else:
+                ve = [value_sum(i, c) for c in range(CHUNKS)]
+                ke = [key_sum(i, c) for c in range(CHUNKS)]
 
             last = i == TILES - 1
-            shared = SHARED[i]
-            own = CHUNKS - shared
-            gate_0 = tile([P, CHUNK], F32, f"listed{max(i, 1) % 2}")
-            gate_rest = tile([P, CHUNKS - 1, CHUNK], F32, f"work{i + 5}" if i + 5 < TILES else f"gate{i % 2}")
-            gate = [gate_0[:]] + [gate_rest[:, c, :] for c in range(CHUNKS - 1)]
-            if shared:
-                value = tile([P, shared, CHUNK], F32, f"value{i % 2}")
-                for c in range(own, CHUNKS):
-                    nc.scalar.copy(value[:, c - own, :], ve[c][:])
+            own = OWN[i]
+            gate = tile([P, J], F32, f"gate{i % 3}")
+            if own < CHUNKS:
+                value = tile([P, J], F32, f"value{i % 2}")
             for c in range(CHUNKS):
                 cols = slice(c * CHUNK, (c + 1) * CHUNK)
-                nc.vector.tensor_tensor(work[:, cols], ke[c][:], work[:, cols], MULT)
-                nc.scalar.activation(gate[c], work[:, cols], SIGMOID)
+                nc.vector.tensor_tensor(state[:, cols], ke[c][:], state[:, cols], MULT)
+                nc.scalar.activation(gate[:, cols], state[:, cols], SIGMOID)
+            for c in range(own, CHUNKS):
+                nc.scalar.copy(value[:, c * CHUNK : (c + 1) * CHUNK], ve[c][:])
             for c in range(own):
                 cols = slice(c * CHUNK, (c + 1) * CHUNK)
-                nc.vector.tensor_tensor(work[:, cols], ve[c][:], gate[c], MULT)
-            if shared:
-                nc.gpsimd.tensor_tensor(
-                    work[:, own * CHUNK :],
-                    value[:].rearrange("p c j -> p (c j)"),
-                    gate_rest[:, own - 1 :, :].rearrange("p c j -> p (c j)"),
-                    MULT,
-                )
+                nc.vector.tensor_tensor(gate[:, cols], ve[c][:], gate[:, cols], MULT)
+            pieces = ((0, 2), (2, CHUNKS)) if own == 0 else ((own, CHUNKS),)
+            for c0, c1 in pieces:
+                if c0 < c1:
+                    cols = slice(c0 * CHUNK, c1 * CHUNK)
+                    nc.gpsimd.tensor_tensor(gate[:, cols], value[:, cols], gate[:, cols], MULT)
 
-            if i > 0:
-                listed = tile([P, J], F32, f"listed{i % 2}")
+            result = state
             if not last:
-                if i > 0:
-                    nc.vector.tensor_copy(listed[:], record[:].indirect(offsets[:]))
-                nc.gpsimd.tensor_tensor(work[:], work[:], listed[:], ADD)
-                stores.append((out[rows, :], work[:]))
+                for h in range(2):
+                    nc.vector.tensor_copy(
+                        result[:, h * J // 2 : (h + 1) * J // 2],
+                        record[:].indirect(offsets[:, 2 * h * step : 2 * (h + 1) * step]),
+                    )
+                nc.gpsimd.tensor_tensor(result, result, gate[:], ADD)
+                stores.append((out[rows, :], result))
             else:
                 for dst, src in stores:
                     nc.sync.dma_start(out=dst, in_=src)
-                step = LIST_COLS // CHUNKS
                 for c in range(CHUNKS):
                     cols = slice(c * CHUNK, (c + 1) * CHUNK)
-                    nc.vector.tensor_copy(listed[:, cols], record[:].indirect(offsets[:, c * step : (c + 1) * step]))
-                    adder = nc.vector if c == CHUNKS - 1 else nc.gpsimd
-                    adder.tensor_tensor(work[:, cols], work[:, cols], listed[:, cols], ADD)
-                    nc.sync.dma_start(out=out[rows, cols], in_=work[:, cols])
+                    listed = record[:].indirect(offsets[:, c * step : (c + 1) * step])
+                    nc.vector.tensor_tensor(result[:, cols], listed, gate[:, cols], ADD)
+                    nc.scalar.dma_start(out=out[rows, cols], in_=result[:, cols])

@@ -49,18 +49,17 @@ def tile_list_engram_qf_sigL_kernel(
         offsets = held.tile([P, LIST_COLS], U16, name="offsets")
         nc.sync.dma_start(offsets[:], offs)
 
-        w_s = tile([P, 3, N], U8, "w_s")
-        nc.vector.memset(w_s[:].rearrange("p a n -> p (a n)").bitcast(I32), 0)
-
-        tab_s = placed([P, T], U8, "tab_s", 140 * KIB)
+        tab_s = placed([P, T], U8, "tab_s", 134 * KIB)
         nc.sync.dma_start(out=tab_s[0:32, :].bitcast(I32), in_=tab_scales.rearrange("a q t -> (a q) t").bitcast(I32))
         nc.vector.memset(tab_s[32:64, :].bitcast(I32), 0)
         nc.vector.memset(tab_s[64:128, :].bitcast(I32), 0)
-        tab_w = placed([P, T], U32, "tab_w", 14 * KIB)
+        tab_w = placed([P, T], U32, "tab_w", 8 * KIB)
         nc.sync.dma_start(out=tab_w[:].bitcast(I32), in_=tab_words[0].rearrange("p t b -> p (t b)").bitcast(I32))
 
         v_s = tile([P, 2, J], U8, "v_s")
         nc.vector.memset(v_s[:].rearrange("p a j -> p (a j)").bitcast(I32), 0)
+        w_s = tile([P, 3, N], U8, "w_s")
+        nc.vector.memset(w_s[:].rearrange("p a n -> p (a n)").bitcast(I32), 0)
 
         for r in range(ROWS):
             nc.gpsimd.dma_start(
@@ -70,16 +69,8 @@ def tile_list_engram_qf_sigL_kernel(
         for r in range(ROWS):
             nc.scalar.dma_start(out=w_s[r:P:32, 2, :].bitcast(I32), in_=wv4_scales[0, r:16:ROWS, :].bitcast(I32))
 
-        wk_rows = wk_words.rearrange("a p n b -> p a (n b)")
-
-        def load_wk(h, words):
-            nc.sync.dma_start(
-                out=words[:].bitcast(I32), in_=wk_rows[:, :, 4 * h * HALF : 4 * (h + 1) * HALF].bitcast(I32)
-            )
-            return words
-
-        state_at = [k * KIB for k in (140, 16, 44, 68, 92, 116, 0, 8)]
-        record_at = [k * KIB for k in (0, 28, 52, 76, 100, 124, 28, 52)]
+        state_at = [k * KIB for k in (128, 24, 56, 80, 104, 136, 0, 32)]
+        record_at = [k * KIB for k in (0, 32, 64, 88, 112, 144, 40, 64)]
 
         def load_st(i):
             state = placed([P, J], F32, f"state{i}", state_at[i])
@@ -91,13 +82,12 @@ def tile_list_engram_qf_sigL_kernel(
             nc.sync.dma_start(out=record[:], in_=rT[i * P : (i + 1) * P, :])
             return record
 
-        raw = placed([P, PACK, N], F32, "raw", 124 * KIB)
-        nc.sync.dma_start(out=raw[:], in_=wv8.rearrange("(p i) n -> p i n", i=PACK))
-        wk_w = [load_wk(0, tile([P, 2, HALF], U32, "wk0"))]
+        wk_w = tile([P, 2, N], U32, "wk_w")
+        nc.sync.dma_start(out=wk_w[:].bitcast(I32), in_=wk_words.rearrange("a p n b -> p a (n b)").bitcast(I32))
         wv4_w = tile([P, 2 * N], U8, "wv4_w")
         nc.sync.dma_start(out=wv4_w[:].bitcast(I32), in_=wv4_words[0].bitcast(I32))
 
-        picked_s = placed([P, J], U8, "picked_s", 156 * KIB)
+        picked_s = placed([P, J], U8, "picked_s", 158 * KIB)
         nc.vector.tensor_copy(picked_s[:], tab_s[:].indirect(offsets[:]))
         for a in range(2):
             for r in range(ROWS):
@@ -105,26 +95,33 @@ def tile_list_engram_qf_sigL_kernel(
                     out=v_s[r:P:32, a, :].bitcast(I32),
                     in_=picked_s[16 * a + r : 16 * (a + 1) : ROWS, :].bitcast(I32),
                 )
+        wv8_rows = wv8.rearrange("(p i) n -> p i n", i=PACK)
+        raw_first = placed([P, PACK, HALF], F32, "raw_first", 136 * KIB + ALIGN)
+        nc.sync.dma_start(out=raw_first[:], in_=wv8_rows[:, :, :HALF])
         state = load_st(0)
 
         wv8_s = tile([P, N], U8, "wv8_s")
         wv8_w = tile([P, N], U32, "wv8_w")
 
-        grouped = placed([P, N, PACK], BF16, "grouped", 148 * KIB)
-        for n0 in range(0, N, QUANT):
-            cols = slice(n0, n0 + QUANT)
-            nc.scalar.copy(grouped[:, cols, :], raw[:, :, cols].rearrange("p i n -> p n i"))
+        grouped = placed([P, N, PACK], BF16, "grouped", 48 * KIB)
+
+        def quantize(cols):
             nc.vector.quantize_mx(
                 out=wv8_w[:, cols].bitcast(FP8X4),
                 scales=wv8_s[:, cols],
                 in_=grouped[:, cols, :].rearrange("p n i -> p (n i)"),
             )
 
+        for n0 in range(0, HALF, QUANT):
+            cols = slice(n0, n0 + QUANT)
+            nc.scalar.copy(grouped[:, cols, :], raw_first[:, :, cols].rearrange("p i n -> p n i"))
+            quantize(cols)
+
         v_w = tile([P, 2, 2 * J], U8, "v_w")
         step = LIST_COLS // CHUNKS
         picked_w = []
         for c in range(CHUNKS):
-            picked = placed([P, CHUNK], U32, f"picked{c}", record_at[c + 2] - KIB if c < CHUNKS - 1 else state_at[5])
+            picked = placed([P, CHUNK], U32, f"picked{c}", record_at[c + 1] - KIB)
             nc.vector.tensor_copy(picked[:], tab_w[:].indirect(offsets[:, c * step : (c + 1) * step]))
             picked_w.append(picked)
         for c in range(CHUNKS):
@@ -132,6 +129,11 @@ def tile_list_engram_qf_sigL_kernel(
                 v_w[:].bitcast(U16)[:, :, c * CHUNK : (c + 1) * CHUNK],
                 picked_w[c][:].bitcast(U16).rearrange("p (j d) -> p d j", d=2),
             )
+
+        raw_rest = placed([P, PACK, HALF], F32, "raw_rest", 16 * KIB)
+        nc.sync.dma_start(out=raw_rest[:], in_=wv8_rows[:, :, HALF:])
+        nc.gpsimd.tensor_scalar(grouped[:, HALF:, :], raw_rest[:].rearrange("p i n -> p n i"), 1.0, 0.0, MULT, ADD)
+        quantize(slice(HALF, N))
 
         def moving(a, c):
             return dict(
@@ -141,7 +143,7 @@ def tile_list_engram_qf_sigL_kernel(
 
         def value_sum(i, c):
             rows = slice(i * P, (i + 1) * P)
-            bank = psum.tile([P, CHUNK], F32, name=f"bank{c + CHUNKS * (i % 2)}")
+            bank = psum.tile([P, CHUNK], F32, name=f"bank{c + CHUNKS * (max(i, 1) % 2)}")
             nc.tensor.matmul_mx(
                 out=bank[:],
                 lhsT=wv8_w[:, rows].bitcast(FP8X4),
@@ -161,12 +163,11 @@ def tile_list_engram_qf_sigL_kernel(
             return bank
 
         def key_sum(i, c):
-            h, c0 = divmod(i * P, HALF)
             bank = psum.tile([P, CHUNK], F32, name=f"bank{c + CHUNKS * ((i + 1) % 2)}")
             for a in range(2):
                 nc.tensor.matmul_mx(
                     out=bank[:],
-                    lhsT=wk_w[h][:, a, c0 : c0 + P].bitcast(FP8X4),
+                    lhsT=wk_w[:, a, i * P : (i + 1) * P].bitcast(FP8X4),
                     lhsT_scale=w_s[:, a, i * P : (i + 1) * P],
                     start=(a == 0),
                     stop=(a == 1),
@@ -180,8 +181,6 @@ def tile_list_engram_qf_sigL_kernel(
             if i > 0:
                 state = load_st(i)
             record = load_record(i)
-            if i == 3:
-                wk_w.append(load_wk(1, placed([P, 2, HALF], U32, "wk1", 24 * KIB)))
 
             if i == 0:
                 ke = [key_sum(i, c) for c in range(CHUNKS)]
@@ -192,7 +191,7 @@ def tile_list_engram_qf_sigL_kernel(
 
             last = i == TILES - 1
             own = OWN[i]
-            gate = tile([P, J], F32, f"gate{i % 3}")
+            gate = tile([P, J], F32, f"gate{i % 4}")
             if own < CHUNKS:
                 value = tile([P, J], F32, f"value{i % 2}")
             for c in range(CHUNKS):
@@ -217,7 +216,9 @@ def tile_list_engram_qf_sigL_kernel(
                         result[:, h * J // 2 : (h + 1) * J // 2],
                         record[:].indirect(offsets[:, 2 * h * step : 2 * (h + 1) * step]),
                     )
-                nc.gpsimd.tensor_tensor(result, result, gate[:], ADD)
+                cut = (own or 2) * CHUNK
+                for cols in (slice(0, cut), slice(cut, J)):
+                    nc.gpsimd.tensor_tensor(result[:, cols], result[:, cols], gate[:, cols], ADD)
                 stores.append((out[rows, :], result))
             else:
                 for dst, src in stores:

@@ -49,6 +49,9 @@ def tile_list_engram_qf_sigL_kernel(
         offsets = held.tile([P, LIST_COLS], U16, name="offsets")
         nc.sync.dma_start(offsets[:], offs)
 
+        w_s = tile([P, 3, N], U8, "w_s")
+        nc.gpsimd.memset(w_s[:].rearrange("p a n -> p (a n)").bitcast(I32), 0)
+
         tab_s = placed([P, T], U8, "tab_s", 134 * KIB)
         nc.sync.dma_start(out=tab_s[0:32, :].bitcast(I32), in_=tab_scales.rearrange("a q t -> (a q) t").bitcast(I32))
         nc.vector.memset(tab_s[32:64, :].bitcast(I32), 0)
@@ -58,8 +61,6 @@ def tile_list_engram_qf_sigL_kernel(
 
         v_s = tile([P, 2, J], U8, "v_s")
         nc.vector.memset(v_s[:].rearrange("p a j -> p (a j)").bitcast(I32), 0)
-        w_s = tile([P, 3, N], U8, "w_s")
-        nc.vector.memset(w_s[:].rearrange("p a n -> p (a n)").bitcast(I32), 0)
 
         for r in range(ROWS):
             nc.gpsimd.dma_start(
@@ -89,16 +90,22 @@ def tile_list_engram_qf_sigL_kernel(
 
         picked_s = placed([P, J], U8, "picked_s", 158 * KIB)
         nc.vector.tensor_copy(picked_s[:], tab_s[:].indirect(offsets[:]))
-        for a in range(2):
-            for r in range(ROWS):
-                nc.scalar.dma_start(
-                    out=v_s[r:P:32, a, :].bitcast(I32),
-                    in_=picked_s[16 * a + r : 16 * (a + 1) : ROWS, :].bitcast(I32),
-                )
+
+        def move_scales(a, r):
+            nc.sync.dma_start(
+                out=v_s[r:P:32, a, :].bitcast(I32),
+                in_=picked_s[16 * a + r : 16 * (a + 1) : ROWS, :].bitcast(I32),
+            )
+
+        moves = [(a, r) for a in range(2) for r in range(ROWS)]
         wv8_rows = wv8.rearrange("(p i) n -> p i n", i=PACK)
+        move_scales(*moves[0])
         raw_first = placed([P, PACK, HALF], F32, "raw_first", 136 * KIB + ALIGN)
         nc.sync.dma_start(out=raw_first[:], in_=wv8_rows[:, :, :HALF])
+        move_scales(*moves[1])
         state = load_st(0)
+        for a, r in moves[2:]:
+            move_scales(a, r)
 
         wv8_s = tile([P, N], U8, "wv8_s")
         wv8_w = tile([P, N], U32, "wv8_w")
@@ -219,7 +226,10 @@ def tile_list_engram_qf_sigL_kernel(
                 cut = (own or 2) * CHUNK
                 for cols in (slice(0, cut), slice(cut, J)):
                     nc.gpsimd.tensor_tensor(result[:, cols], result[:, cols], gate[:, cols], ADD)
-                stores.append((out[rows, :], result))
+                    if i == TILES - 2:
+                        stores.append((out[rows, cols], result[:, cols]))
+                if i < TILES - 2:
+                    stores.append((out[rows, :], result))
             else:
                 for dst, src in stores:
                     nc.sync.dma_start(out=dst, in_=src)

@@ -1,6 +1,7 @@
 from contextlib import ExitStack
 
 import concourse.mybir as mybir
+from concourse.masks import make_identity
 
 K, N, T, J = 1024, 1024, 4096, 2048
 FLOPS = 2 * 2 * K * N * J
@@ -26,7 +27,8 @@ TILES = N // P
 HALF = N // 2
 QUANT = 256
 LIST_COLS = J // 16
-OWN = (0, 1, 1, 1, 1, 1, 2, 4)
+OWN = (2, 1, 0, 1, 0, 1, 1, 4)
+LAG = 2
 KIB = 1024
 ALIGN = 64
 
@@ -182,7 +184,31 @@ def tile_list_engram_qf_sigL_kernel(
                 )
             return bank
 
+        identity = tile([P, P], F32, "identity")
+        make_identity(nc, identity[:])
+
+        def add_by_transposes(bank, result, gate):
+            blocks = [slice(b * P, (b + 1) * P) for b in range(CHUNK // P)]
+            cols = slice(0, CHUNK)
+            turned = psum.tile([P, CHUNK], F32, name=f"bank{bank}")
+            for b, block in enumerate(blocks):
+                for first, addend in ((True, gate), (False, result)):
+                    nc.tensor.matmul(
+                        turned[:, b * P : (b + 1) * P],
+                        addend[:, block],
+                        identity[:],
+                        start=first,
+                        stop=not first,
+                        is_transpose=True,
+                    )
+            nc.scalar.copy(gate[:, cols], turned[:])
+            back = psum.tile([P, CHUNK], F32, name=f"bank{bank + 1}")
+            for b, block in enumerate(blocks):
+                nc.tensor.transpose(back[:, b * P : (b + 1) * P], gate[:, block], identity[:])
+            nc.scalar.copy(result[:, cols], back[:])
+
         stores = []
+        waiting = []
         for i in range(TILES):
             rows = slice(i * P, (i + 1) * P)
             if i > 0:
@@ -207,10 +233,16 @@ def tile_list_engram_qf_sigL_kernel(
                 nc.scalar.activation(gate[:, cols], state[:, cols], SIGMOID)
             for c in range(own, CHUNKS):
                 nc.scalar.copy(value[:, c * CHUNK : (c + 1) * CHUNK], ve[c][:])
+            if last:
+                for k, addends in enumerate(waiting[i - LAG :]):
+                    add_by_transposes(CHUNKS * ((i + 1) % 2) + 2 * k, *addends)
+            elif i >= LAG:
+                add_by_transposes(CHUNKS * (i % 2) + 1, *waiting[i - LAG])
+            waiting.append((state, gate))
             for c in range(own):
                 cols = slice(c * CHUNK, (c + 1) * CHUNK)
                 nc.vector.tensor_tensor(gate[:, cols], ve[c][:], gate[:, cols], MULT)
-            pieces = ((0, 2), (2, CHUNKS)) if own == 0 else ((own, CHUNKS),)
+            pieces = ((own, 2), (max(own, 2), CHUNKS))
             for c0, c1 in pieces:
                 if c0 < c1:
                     cols = slice(c0 * CHUNK, c1 * CHUNK)
@@ -223,12 +255,12 @@ def tile_list_engram_qf_sigL_kernel(
                         result[:, h * J // 2 : (h + 1) * J // 2],
                         record[:].indirect(offsets[:, 2 * h * step : 2 * (h + 1) * step]),
                     )
-                cut = (own or 2) * CHUNK
-                for cols in (slice(0, cut), slice(cut, J)):
+                for cols in (slice(CHUNK, J // 2), slice(J // 2, J)):
                     nc.gpsimd.tensor_tensor(result[:, cols], result[:, cols], gate[:, cols], ADD)
-                    if i == TILES - 2:
+                if i == TILES - 2:
+                    for cols in (slice(0, J // 2), slice(J // 2, J)):
                         stores.append((out[rows, cols], result[:, cols]))
-                if i < TILES - 2:
+                else:
                     stores.append((out[rows, :], result))
             else:
                 for dst, src in stores:

@@ -27,7 +27,8 @@ TILES = N // P
 HALF = N // 2
 QUANT = 256
 LIST_COLS = J // 16
-OWN = (2, 1, 0, 1, 0, 1, 1, 4)
+OWN = (2, 1, 0, 1, 1, 1, 1, 4)
+TURNED = (1, 1, 1, 1, 1, 0, 1)
 LAG = 2
 KIB = 1024
 ALIGN = 64
@@ -51,9 +52,6 @@ def tile_list_engram_qf_sigL_kernel(
         offsets = held.tile([P, LIST_COLS], U16, name="offsets")
         nc.sync.dma_start(offsets[:], offs)
 
-        w_s = tile([P, 3, N], U8, "w_s")
-        nc.gpsimd.memset(w_s[:].rearrange("p a n -> p (a n)").bitcast(I32), 0)
-
         tab_s = placed([P, T], U8, "tab_s", 134 * KIB)
         nc.sync.dma_start(out=tab_s[0:32, :].bitcast(I32), in_=tab_scales.rearrange("a q t -> (a q) t").bitcast(I32))
         nc.vector.memset(tab_s[32:64, :].bitcast(I32), 0)
@@ -63,6 +61,8 @@ def tile_list_engram_qf_sigL_kernel(
 
         v_s = tile([P, 2, J], U8, "v_s")
         nc.vector.memset(v_s[:].rearrange("p a j -> p (a j)").bitcast(I32), 0)
+        w_s = tile([P, 3, N], U8, "w_s")
+        nc.vector.memset(w_s[:].rearrange("p a n -> p (a n)").bitcast(I32), 0)
 
         for r in range(ROWS):
             nc.gpsimd.dma_start(
@@ -187,10 +187,10 @@ def tile_list_engram_qf_sigL_kernel(
         identity = tile([P, P], F32, "identity")
         make_identity(nc, identity[:])
 
-        def add_by_transposes(bank, result, gate):
-            blocks = [slice(b * P, (b + 1) * P) for b in range(CHUNK // P)]
-            cols = slice(0, CHUNK)
-            turned = psum.tile([P, CHUNK], F32, name=f"bank{bank}")
+        def add_by_transposes(c, banks, result, gate):
+            blocks = [slice(c * CHUNK + b * P, c * CHUNK + (b + 1) * P) for b in range(CHUNK // P)]
+            cols = slice(c * CHUNK, (c + 1) * CHUNK)
+            turned = psum.tile([P, CHUNK], F32, name=f"bank{banks[0]}")
             for b, block in enumerate(blocks):
                 for first, addend in ((True, gate), (False, result)):
                     nc.tensor.matmul(
@@ -202,7 +202,7 @@ def tile_list_engram_qf_sigL_kernel(
                         is_transpose=True,
                     )
             nc.scalar.copy(gate[:, cols], turned[:])
-            back = psum.tile([P, CHUNK], F32, name=f"bank{bank + 1}")
+            back = psum.tile([P, CHUNK], F32, name=f"bank{banks[1]}")
             for b, block in enumerate(blocks):
                 nc.tensor.transpose(back[:, b * P : (b + 1) * P], gate[:, block], identity[:])
             nc.scalar.copy(result[:, cols], back[:])
@@ -234,10 +234,14 @@ def tile_list_engram_qf_sigL_kernel(
             for c in range(own, CHUNKS):
                 nc.scalar.copy(value[:, c * CHUNK : (c + 1) * CHUNK], ve[c][:])
             if last:
-                for k, addends in enumerate(waiting[i - LAG :]):
-                    add_by_transposes(CHUNKS * ((i + 1) % 2) + 2 * k, *addends)
+                for k in range(LAG):
+                    first = CHUNKS * ((i + 1) % 2) + 2 * k
+                    if TURNED[i - 1 - k]:
+                        add_by_transposes(0, (first, first + 1), *waiting[i - 1 - k])
             elif i >= LAG:
-                add_by_transposes(CHUNKS * (i % 2) + 1, *waiting[i - LAG])
+                first = CHUNKS * (i % 2)
+                for c in range(TURNED[i - LAG]):
+                    add_by_transposes(c, (first + 1 + 2 * c, first + 2 - c), *waiting[i - LAG])
             waiting.append((state, gate))
             for c in range(own):
                 cols = slice(c * CHUNK, (c + 1) * CHUNK)
@@ -255,13 +259,11 @@ def tile_list_engram_qf_sigL_kernel(
                         result[:, h * J // 2 : (h + 1) * J // 2],
                         record[:].indirect(offsets[:, 2 * h * step : 2 * (h + 1) * step]),
                     )
-                for cols in (slice(CHUNK, J // 2), slice(J // 2, J)):
-                    nc.gpsimd.tensor_tensor(result[:, cols], result[:, cols], gate[:, cols], ADD)
-                if i == TILES - 2:
-                    for cols in (slice(0, J // 2), slice(J // 2, J)):
-                        stores.append((out[rows, cols], result[:, cols]))
-                else:
-                    stores.append((out[rows, :], result))
+                for c0, c1 in ((TURNED[i], 2), (2, CHUNKS)):
+                    if c0 < c1:
+                        cols = slice(c0 * CHUNK, c1 * CHUNK)
+                        nc.gpsimd.tensor_tensor(result[:, cols], result[:, cols], gate[:, cols], ADD)
+                stores.append((out[rows, :], result))
             else:
                 for dst, src in stores:
                     nc.sync.dma_start(out=dst, in_=src)
@@ -269,4 +271,6 @@ def tile_list_engram_qf_sigL_kernel(
                     cols = slice(c * CHUNK, (c + 1) * CHUNK)
                     listed = record[:].indirect(offsets[:, c * step : (c + 1) * step])
                     nc.vector.tensor_tensor(result[:, cols], listed, gate[:, cols], ADD)
-                    nc.scalar.dma_start(out=out[rows, cols], in_=result[:, cols])
+                    if c % 2:
+                        half = slice((c - 1) * CHUNK, (c + 1) * CHUNK)
+                        nc.scalar.dma_start(out=out[rows, half], in_=result[:, half])

@@ -62,7 +62,7 @@ def tile_list_engram_qf_sigL_kernel(
         v_s = tile([P, 2, J], U8, "v_s")
         nc.vector.memset(v_s[:].rearrange("p a j -> p (a j)").bitcast(I32), 0)
         w_s = tile([P, 3, N], U8, "w_s")
-        nc.vector.memset(w_s[:].rearrange("p a n -> p (a n)").bitcast(I32), 0)
+        nc.gpsimd.memset(w_s[:].rearrange("p a n -> p (a n)").bitcast(I32), 0)
 
         for r in range(ROWS):
             nc.gpsimd.dma_start(
@@ -70,7 +70,7 @@ def tile_list_engram_qf_sigL_kernel(
                 in_=wk_scales[:, r:16:ROWS, :].rearrange("a q n -> q a n").bitcast(I32),
             )
         for r in range(ROWS):
-            nc.scalar.dma_start(out=w_s[r:P:32, 2, :].bitcast(I32), in_=wv4_scales[0, r:16:ROWS, :].bitcast(I32))
+            nc.gpsimd.dma_start(out=w_s[r:P:32, 2, :].bitcast(I32), in_=wv4_scales[0, r:16:ROWS, :].bitcast(I32))
 
         state_at = [k * KIB for k in (128, 24, 56, 80, 104, 136, 0, 32)]
         record_at = [k * KIB for k in (0, 32, 64, 88, 112, 144, 40, 64)]
@@ -85,6 +85,9 @@ def tile_list_engram_qf_sigL_kernel(
             nc.sync.dma_start(out=record[:], in_=rT[i * P : (i + 1) * P, :])
             return record
 
+        wv8_rows = wv8.rearrange("(p i) n -> p i n", i=PACK)
+        raw_first = placed([P, PACK, HALF], F32, "raw_first", 146 * KIB)
+        nc.sync.dma_start(out=raw_first[:], in_=wv8_rows[:, :, :HALF])
         wk_w = tile([P, 2, N], U32, "wk_w")
         nc.sync.dma_start(out=wk_w[:].bitcast(I32), in_=wk_words.rearrange("a p n b -> p a (n b)").bitcast(I32))
         wv4_w = tile([P, 2 * N], U8, "wv4_w")
@@ -100,14 +103,13 @@ def tile_list_engram_qf_sigL_kernel(
             )
 
         moves = [(a, r) for a in range(2) for r in range(ROWS)]
-        wv8_rows = wv8.rearrange("(p i) n -> p i n", i=PACK)
-        move_scales(*moves[0])
-        raw_first = placed([P, PACK, HALF], F32, "raw_first", 136 * KIB + ALIGN)
-        nc.sync.dma_start(out=raw_first[:], in_=wv8_rows[:, :, :HALF])
-        move_scales(*moves[1])
-        state = load_st(0)
-        for a, r in moves[2:]:
+        for a, r in moves[:5]:
             move_scales(a, r)
+        raw_rest = placed([P, PACK, HALF], F32, "raw_rest", 136 * KIB + ALIGN)
+        nc.sync.dma_start(out=raw_rest[:], in_=wv8_rows[:, :, HALF:])
+        for a, r in moves[5:]:
+            move_scales(a, r)
+        state = load_st(0)
 
         wv8_s = tile([P, N], U8, "wv8_s")
         wv8_w = tile([P, N], U32, "wv8_w")
@@ -139,8 +141,6 @@ def tile_list_engram_qf_sigL_kernel(
                 picked_w[c][:].bitcast(U16).rearrange("p (j d) -> p d j", d=2),
             )
 
-        raw_rest = placed([P, PACK, HALF], F32, "raw_rest", 16 * KIB)
-        nc.sync.dma_start(out=raw_rest[:], in_=wv8_rows[:, :, HALF:])
         nc.gpsimd.tensor_scalar(grouped[:, HALF:, :], raw_rest[:].rearrange("p i n -> p n i"), 1.0, 0.0, MULT, ADD)
         quantize(slice(HALF, N))
 

@@ -52,7 +52,7 @@ def tile_list_engram_qf_sigL_kernel(
         offsets = held.tile([P, LIST_COLS], U16, name="offsets")
         nc.sync.dma_start(offsets[:], offs)
 
-        tab_s = placed([P, T], U8, "tab_s", 134 * KIB)
+        tab_s = placed([P, T], U8, "tab_s", 135 * KIB)
         nc.sync.dma_start(out=tab_s[0:32, :].bitcast(I32), in_=tab_scales.rearrange("a q t -> (a q) t").bitcast(I32))
         nc.vector.memset(tab_s[32:64, :].bitcast(I32), 0)
         nc.vector.memset(tab_s[64:128, :].bitcast(I32), 0)
@@ -61,19 +61,21 @@ def tile_list_engram_qf_sigL_kernel(
 
         v_s = tile([P, 2, J], U8, "v_s")
         nc.vector.memset(v_s[:].rearrange("p a j -> p (a j)").bitcast(I32), 0)
-        w_s = tile([P, 3, N], U8, "w_s")
-        nc.gpsimd.memset(w_s[:].rearrange("p a n -> p (a n)").bitcast(I32), 0)
+        wk_s = tile([P, 2, N], U8, "wk_s")
+        nc.gpsimd.memset(wk_s[:].rearrange("p a n -> p (a n)").bitcast(I32), 0)
+        wv4_s = tile([P, N], U8, "wv4_s")
+        nc.vector.memset(wv4_s[:].bitcast(I32), 0)
 
         for r in range(ROWS):
             nc.gpsimd.dma_start(
-                out=w_s[r:P:32, 0:2, :].bitcast(I32),
+                out=wk_s[r:P:32, :, :].bitcast(I32),
                 in_=wk_scales[:, r:16:ROWS, :].rearrange("a q n -> q a n").bitcast(I32),
             )
         for r in range(ROWS):
-            nc.gpsimd.dma_start(out=w_s[r:P:32, 2, :].bitcast(I32), in_=wv4_scales[0, r:16:ROWS, :].bitcast(I32))
+            nc.gpsimd.dma_start(out=wv4_s[r:P:32, :].bitcast(I32), in_=wv4_scales[0, r:16:ROWS, :].bitcast(I32))
 
-        state_at = [k * KIB for k in (128, 24, 56, 80, 104, 136, 0, 32)]
-        record_at = [k * KIB for k in (0, 32, 64, 88, 112, 144, 40, 64)]
+        state_at = [k * KIB for k in (138, 24, 56, 80, 104, 146, 0, 32)]
+        record_at = [k * KIB for k in (0, 32, 64, 88, 112, 154, 40, 64)]
 
         def load_st(i):
             state = placed([P, J], F32, f"state{i}", state_at[i])
@@ -85,15 +87,10 @@ def tile_list_engram_qf_sigL_kernel(
             nc.sync.dma_start(out=record[:], in_=rT[i * P : (i + 1) * P, :])
             return record
 
-        wv8_rows = wv8.rearrange("(p i) n -> p i n", i=PACK)
-        raw_first = placed([P, PACK, HALF], F32, "raw_first", 146 * KIB)
-        nc.sync.dma_start(out=raw_first[:], in_=wv8_rows[:, :, :HALF])
-        wk_w = tile([P, 2, N], U32, "wk_w")
-        nc.sync.dma_start(out=wk_w[:].bitcast(I32), in_=wk_words.rearrange("a p n b -> p a (n b)").bitcast(I32))
-        wv4_w = tile([P, 2 * N], U8, "wv4_w")
-        nc.sync.dma_start(out=wv4_w[:].bitcast(I32), in_=wv4_words[0].bitcast(I32))
+        raw = placed([P, PACK, N], F32, "raw", 146 * KIB)
+        nc.sync.dma_start(out=raw[:], in_=wv8.rearrange("(p i) n -> p i n", i=PACK))
 
-        picked_s = placed([P, J], U8, "picked_s", 158 * KIB)
+        picked_s = placed([P, J], U8, "picked_s", 168 * KIB)
         nc.vector.tensor_copy(picked_s[:], tab_s[:].indirect(offsets[:]))
 
         def move_scales(a, r):
@@ -105,8 +102,10 @@ def tile_list_engram_qf_sigL_kernel(
         moves = [(a, r) for a in range(2) for r in range(ROWS)]
         for a, r in moves[:5]:
             move_scales(a, r)
-        raw_rest = placed([P, PACK, HALF], F32, "raw_rest", 136 * KIB + ALIGN)
-        nc.sync.dma_start(out=raw_rest[:], in_=wv8_rows[:, :, HALF:])
+        wk_w = placed([P, 2, N], U32, "wk_w", 128 * KIB)
+        nc.sync.dma_start(out=wk_w[:].bitcast(I32), in_=wk_words.rearrange("a p n b -> p a (n b)").bitcast(I32))
+        wv4_w = placed([P, 2 * N], U8, "wv4_w", 136 * KIB)
+        nc.sync.dma_start(out=wv4_w[:].bitcast(I32), in_=wv4_words[0].bitcast(I32))
         for a, r in moves[5:]:
             move_scales(a, r)
         state = load_st(0)
@@ -125,7 +124,7 @@ def tile_list_engram_qf_sigL_kernel(
 
         for n0 in range(0, HALF, QUANT):
             cols = slice(n0, n0 + QUANT)
-            nc.scalar.copy(grouped[:, cols, :], raw_first[:, :, cols].rearrange("p i n -> p n i"))
+            nc.scalar.copy(grouped[:, cols, :], raw[:, :, cols].rearrange("p i n -> p n i"))
             quantize(cols)
 
         v_w = tile([P, 2, 2 * J], U8, "v_w")
@@ -141,7 +140,7 @@ def tile_list_engram_qf_sigL_kernel(
                 picked_w[c][:].bitcast(U16).rearrange("p (j d) -> p d j", d=2),
             )
 
-        nc.gpsimd.tensor_scalar(grouped[:, HALF:, :], raw_rest[:].rearrange("p i n -> p n i"), 1.0, 0.0, MULT, ADD)
+        nc.gpsimd.tensor_scalar(grouped[:, HALF:, :], raw[:, :, HALF:].rearrange("p i n -> p n i"), 1.0, 0.0, MULT, ADD)
         quantize(slice(HALF, N))
 
         def moving(a, c):
@@ -164,7 +163,7 @@ def tile_list_engram_qf_sigL_kernel(
             nc.tensor.matmul_mx(
                 out=bank[:],
                 lhsT=wv4_w[:, 2 * i * P : 2 * (i + 1) * P].bitcast(FP4X4),
-                lhsT_scale=w_s[:, 2, rows],
+                lhsT_scale=wv4_s[:, rows],
                 start=False,
                 stop=True,
                 **moving(1, c),
@@ -177,7 +176,7 @@ def tile_list_engram_qf_sigL_kernel(
                 nc.tensor.matmul_mx(
                     out=bank[:],
                     lhsT=wk_w[:, a, i * P : (i + 1) * P].bitcast(FP8X4),
-                    lhsT_scale=w_s[:, a, i * P : (i + 1) * P],
+                    lhsT_scale=wk_s[:, a, i * P : (i + 1) * P],
                     start=(a == 0),
                     stop=(a == 1),
                     **moving(a, c),

@@ -30,6 +30,7 @@ LIST_COLS = J // 16
 OWN = (2, 1, 0, 1, 1, 1, 1, 4)
 TURNED = (1, 1, 1, 1, 1, 0, 1)
 LAG = 2
+SCALE_ROWS_AT = (48, 112)
 KIB = 1024
 ALIGN = 64
 
@@ -53,14 +54,18 @@ def tile_list_engram_qf_sigL_kernel(
         nc.sync.dma_start(offsets[:], offs)
 
         tab_s = placed([P, T], U8, "tab_s", 135 * KIB)
-        nc.sync.dma_start(out=tab_s[0:32, :].bitcast(I32), in_=tab_scales.rearrange("a q t -> (a q) t").bitcast(I32))
-        nc.vector.memset(tab_s[32:64, :].bitcast(I32), 0)
-        nc.vector.memset(tab_s[64:128, :].bitcast(I32), 0)
+        for a in range(2):
+            nc.sync.dma_start(
+                out=tab_s[SCALE_ROWS_AT[a] : SCALE_ROWS_AT[a] + 16, :].bitcast(I32), in_=tab_scales[a].bitcast(I32)
+            )
+        for p0, p1 in ((0, 48), (64, 112)):
+            nc.vector.memset(tab_s[p0:p1, :].bitcast(I32), 0)
         tab_w = placed([P, T], U32, "tab_w", 8 * KIB)
         nc.sync.dma_start(out=tab_w[:].bitcast(I32), in_=tab_words[0].rearrange("p t b -> p (t b)").bitcast(I32))
 
-        v_s = tile([P, 2, J], U8, "v_s")
-        nc.vector.memset(v_s[:].rearrange("p a j -> p (a j)").bitcast(I32), 0)
+        v_s = [tile([P, J], U8, f"v_s{a}") for a in range(2)]
+        for plane in v_s:
+            nc.vector.memset(plane[:].bitcast(I32), 0)
         wk_s = tile([P, 2, N], U8, "wk_s")
         nc.gpsimd.memset(wk_s[:].rearrange("p a n -> p (a n)").bitcast(I32), 0)
         wv4_s = tile([P, N], U8, "wv4_s")
@@ -90,25 +95,32 @@ def tile_list_engram_qf_sigL_kernel(
         raw = placed([P, PACK, N], F32, "raw", 146 * KIB)
         nc.sync.dma_start(out=raw[:], in_=wv8.rearrange("(p i) n -> p i n", i=PACK))
 
-        picked_s = placed([P, J], U8, "picked_s", 168 * KIB)
+        picked_s = placed([P, J], U8, "picked_s", 127 * KIB)
         nc.vector.tensor_copy(picked_s[:], tab_s[:].indirect(offsets[:]))
 
         def move_scales(a, r):
             nc.sync.dma_start(
-                out=v_s[r:P:32, a, :].bitcast(I32),
-                in_=picked_s[16 * a + r : 16 * (a + 1) : ROWS, :].bitcast(I32),
+                out=v_s[a][r:P:32, :].bitcast(I32),
+                in_=picked_s[SCALE_ROWS_AT[a] + r : SCALE_ROWS_AT[a] + 16 : ROWS, :].bitcast(I32),
             )
 
+        def load_key_words(h, offset):
+            words = placed([P, 2, HALF], U32, f"wk_w{h}", offset)
+            nc.sync.dma_start(
+                out=words[:].bitcast(I32),
+                in_=wk_words[:, :, h * HALF : (h + 1) * HALF, :].rearrange("a p n b -> p a (n b)").bitcast(I32),
+            )
+            return words
+
         moves = [(a, r) for a in range(2) for r in range(ROWS)]
-        for a, r in moves[:5]:
+        for a, r in moves[:ROWS]:
             move_scales(a, r)
-        wk_w = placed([P, 2, N], U32, "wk_w", 128 * KIB)
-        nc.sync.dma_start(out=wk_w[:].bitcast(I32), in_=wk_words.rearrange("a p n b -> p a (n b)").bitcast(I32))
+        wk_w = [load_key_words(0, 132 * KIB)]
         wv4_w = placed([P, 2 * N], U8, "wv4_w", 136 * KIB)
         nc.sync.dma_start(out=wv4_w[:].bitcast(I32), in_=wv4_words[0].bitcast(I32))
-        for a, r in moves[5:]:
-            move_scales(a, r)
         state = load_st(0)
+        for a, r in moves[ROWS:]:
+            move_scales(a, r)
 
         wv8_s = tile([P, N], U8, "wv8_s")
         wv8_w = tile([P, N], U32, "wv8_w")
@@ -146,7 +158,7 @@ def tile_list_engram_qf_sigL_kernel(
         def moving(a, c):
             return dict(
                 rhs=v_w[:, a, 2 * c * CHUNK : 2 * (c + 1) * CHUNK].bitcast(FP4X4),
-                rhs_scale=v_s[:, a, c * CHUNK : (c + 1) * CHUNK],
+                rhs_scale=v_s[a][:, c * CHUNK : (c + 1) * CHUNK],
             )
 
         def value_sum(i, c):
@@ -175,7 +187,7 @@ def tile_list_engram_qf_sigL_kernel(
             for a in range(2):
                 nc.tensor.matmul_mx(
                     out=bank[:],
-                    lhsT=wk_w[:, a, i * P : (i + 1) * P].bitcast(FP8X4),
+                    lhsT=wk_w[i * P // HALF][:, a, i * P % HALF : i * P % HALF + P].bitcast(FP8X4),
                     lhsT_scale=wk_s[:, a, i * P : (i + 1) * P],
                     start=(a == 0),
                     stop=(a == 1),
@@ -213,6 +225,8 @@ def tile_list_engram_qf_sigL_kernel(
             if i > 0:
                 state = load_st(i)
             record = load_record(i)
+            if i == 2:
+                wk_w.append(load_key_words(1, 128 * KIB))
 
             if i == 0:
                 ke = [key_sum(i, c) for c in range(CHUNKS)]

@@ -252,9 +252,9 @@ def tile_list_engram_qf_sigL_kernel(
                     if TURNED[i - 1 - k]:
                         add_by_transposes(0, (first, first + 1), *waiting[i - 1 - k])
             elif i >= LAG:
-                first = CHUNKS * (i % 2)
+                first = CHUNKS * ((i + 1) % 2)
                 for c in range(TURNED[i - LAG]):
-                    add_by_transposes(c, (first + 1 + 2 * c, first + 2 - c), *waiting[i - LAG])
+                    add_by_transposes(c, (first, first + 1), *waiting[i - LAG])
             waiting.append((state, gate))
             for c in range(own):
                 cols = slice(c * CHUNK, (c + 1) * CHUNK)

@@ -28,7 +28,7 @@ HALF = N // 2
 QUANT = 256
 LIST_COLS = J // 16
 OWN = (2, 1, 0, 1, 1, 1, 1, 4)
-TURNED = (1, 1, 1, 1, 1, 0, 1)
+TURNED = (1, 1, 1, 1, 1, 0, 2)
 LAG = 2
 SCALE_ROWS_AT = (48, 112)
 KIB = 1024
@@ -247,10 +247,9 @@ def tile_list_engram_qf_sigL_kernel(
             for c in range(own, CHUNKS):
                 nc.scalar.copy(value[:, c * CHUNK : (c + 1) * CHUNK], ve[c][:])
             if last:
-                for k in range(LAG):
-                    first = CHUNKS * ((i + 1) % 2) + 2 * k
-                    if TURNED[i - 1 - k]:
-                        add_by_transposes(0, (first, first + 1), *waiting[i - 1 - k])
+                for c in range(TURNED[i - 1]):
+                    first = CHUNKS * ((i + 1) % 2) + 2 * c
+                    add_by_transposes(c, (first, first + 1), *waiting[i - 1])
             elif i >= LAG:
                 first = CHUNKS * ((i + 1) % 2)
                 for c in range(TURNED[i - LAG]):
@@ -284,6 +283,6 @@ def tile_list_engram_qf_sigL_kernel(
                     cols = slice(c * CHUNK, (c + 1) * CHUNK)
                     listed = record[:].indirect(offsets[:, c * step : (c + 1) * step])
                     nc.vector.tensor_tensor(result[:, cols], listed, gate[:, cols], ADD)
-                    if c % 2:
-                        half = slice((c - 1) * CHUNK, (c + 1) * CHUNK)
-                        nc.scalar.dma_start(out=out[rows, half], in_=result[:, half])
+                    if c > 0:
+                        done = slice(0, 2 * CHUNK) if c == 1 else cols
+                        nc.scalar.dma_start(out=out[rows, done], in_=result[:, done])

@@ -27,7 +27,7 @@ TILES = N // P
 HALF = N // 2
 QUANT = 256
 LIST_COLS = J // 16
-OWN = (2, 1, 0, 1, 1, 1, 1, 4)
+OWN = (2, 1, 1, 1, 1, 1, 1, 4)
 TURNED = (1, 1, 1, 1, 1, 0, 2)
 LAG = 2
 SCALE_ROWS_AT = (48, 112)
@@ -65,11 +65,12 @@ def tile_list_engram_qf_sigL_kernel(
 
         v_s = [tile([P, J], U8, f"v_s{a}") for a in range(2)]
         for plane in v_s:
-            nc.vector.memset(plane[:].bitcast(I32), 0)
+            for words in (slice(0, J // 8 + 1), slice(J // 8 + 1, J // 4)):
+                nc.vector.memset(plane[:].bitcast(I32)[:, words], 0)
         wk_s = tile([P, 2, N], U8, "wk_s")
         nc.gpsimd.memset(wk_s[:].rearrange("p a n -> p (a n)").bitcast(I32), 0)
         wv4_s = tile([P, N], U8, "wv4_s")
-        nc.vector.memset(wv4_s[:].bitcast(I32), 0)
+        nc.gpsimd.memset(wv4_s[:].bitcast(I32), 0)
 
         for r in range(ROWS):
             nc.gpsimd.dma_start(

@@ -153,7 +153,7 @@ def tile_list_engram_qf_sigL_kernel(
                 picked_w[c][:].bitcast(U16).rearrange("p (j d) -> p d j", d=2),
             )
 
-        nc.gpsimd.tensor_scalar(grouped[:, HALF:, :], raw[:, :, HALF:].rearrange("p i n -> p n i"), 1.0, 0.0, MULT, ADD)
+        nc.vector.tensor_copy(grouped[:, HALF:, :], raw[:, :, HALF:].rearrange("p i n -> p n i"))
         quantize(slice(HALF, N))
 
         def moving(a, c):

@@ -30,7 +30,7 @@ LIST_COLS = J // 16
 OWN = (2, 1, 1, 1, 1, 1, 1, 4)
 TURNED = (1, 1, 1, 1, 1, 0, 2)
 LAG = 2
-SCALE_ROWS_AT = (48, 112)
+SCALE_ROWS_AT = (96, 112)
 KIB = 1024
 ALIGN = 64
 
@@ -54,12 +54,10 @@ def tile_list_engram_qf_sigL_kernel(
         nc.sync.dma_start(offsets[:], offs)
 
         tab_s = placed([P, T], U8, "tab_s", 135 * KIB)
-        for a in range(2):
-            nc.sync.dma_start(
-                out=tab_s[SCALE_ROWS_AT[a] : SCALE_ROWS_AT[a] + 16, :].bitcast(I32), in_=tab_scales[a].bitcast(I32)
-            )
-        for p0, p1 in ((0, 48), (64, 112)):
-            nc.vector.memset(tab_s[p0:p1, :].bitcast(I32), 0)
+        nc.sync.dma_start(
+            out=tab_s[SCALE_ROWS_AT[0] :, :].bitcast(I32), in_=tab_scales.rearrange("a q t -> (a q) t").bitcast(I32)
+        )
+        nc.vector.memset(tab_s[: SCALE_ROWS_AT[0], :].bitcast(I32), 0)
         tab_w = placed([P, T], U32, "tab_w", 8 * KIB)
         nc.sync.dma_start(out=tab_w[:].bitcast(I32), in_=tab_words[0].rearrange("p t b -> p (t b)").bitcast(I32))
 
@@ -284,6 +282,6 @@ def tile_list_engram_qf_sigL_kernel(
                     cols = slice(c * CHUNK, (c + 1) * CHUNK)
                     listed = record[:].indirect(offsets[:, c * step : (c + 1) * step])
                     nc.vector.tensor_tensor(result[:, cols], listed, gate[:, cols], ADD)
-                    if c > 0:
-                        done = slice(0, 2 * CHUNK) if c == 1 else cols
+                    if c % 2 == 1:
+                        done = slice((c - 1) * CHUNK, (c + 1) * CHUNK)
                         nc.scalar.dma_start(out=out[rows, done], in_=result[:, done])

@@ -53,7 +53,7 @@ def tile_list_engram_qf_sigL_kernel(
         offsets = held.tile([P, LIST_COLS], U16, name="offsets")
         nc.sync.dma_start(offsets[:], offs)
 
-        tab_s = placed([P, T], U8, "tab_s", 135 * KIB)
+        tab_s = placed([P, T], U8, "tab_s", 136 * KIB)
         nc.sync.dma_start(
             out=tab_s[SCALE_ROWS_AT[0] :, :].bitcast(I32), in_=tab_scales.rearrange("a q t -> (a q) t").bitcast(I32)
         )
@@ -94,6 +94,9 @@ def tile_list_engram_qf_sigL_kernel(
         raw = placed([P, PACK, N], F32, "raw", 146 * KIB)
         nc.sync.dma_start(out=raw[:], in_=wv8.rearrange("(p i) n -> p i n", i=PACK))
 
+        wv4_w = placed([P, 2 * N], U8, "wv4_w", 132 * KIB)
+        nc.sync.dma_start(out=wv4_w[:].bitcast(I32), in_=wv4_words[0].bitcast(I32))
+
         picked_s = placed([P, J], U8, "picked_s", 127 * KIB)
         nc.vector.tensor_copy(picked_s[:], tab_s[:].indirect(offsets[:]))
 
@@ -114,9 +117,7 @@ def tile_list_engram_qf_sigL_kernel(
         moves = [(a, r) for a in range(2) for r in range(ROWS)]
         for a, r in moves[:ROWS]:
             move_scales(a, r)
-        wk_w = [load_key_words(0, 132 * KIB)]
-        wv4_w = placed([P, 2 * N], U8, "wv4_w", 136 * KIB)
-        nc.sync.dma_start(out=wv4_w[:].bitcast(I32), in_=wv4_words[0].bitcast(I32))
+        wk_w = [load_key_words(0, 134 * KIB)]
         state = load_st(0)
         for a, r in moves[ROWS:]:
             move_scales(a, r)

@@ -283,6 +283,6 @@ def tile_list_engram_qf_sigL_kernel(
                     cols = slice(c * CHUNK, (c + 1) * CHUNK)
                     listed = record[:].indirect(offsets[:, c * step : (c + 1) * step])
                     nc.vector.tensor_tensor(result[:, cols], listed, gate[:, cols], ADD)
-                    if c % 2 == 1:
-                        done = slice((c - 1) * CHUNK, (c + 1) * CHUNK)
+                    if c > 0:
+                        done = slice(0, 2 * CHUNK) if c == 1 else cols
                         nc.scalar.dma_start(out=out[rows, done], in_=result[:, done])

from contextlib import ExitStack

import concourse.mybir as mybir
from concourse.masks import make_identity

K, N, T, J = 1024, 1024, 4096, 2048
FLOPS = 2 * 2 * K * N * J

F32 = mybir.dt.float32
BF16 = mybir.dt.bfloat16
I32 = mybir.dt.int32
U32 = mybir.dt.uint32
U16 = mybir.dt.uint16
U8 = mybir.dt.uint8
FP8X4 = mybir.dt.float8_e4m3fn_x4
FP4X4 = mybir.dt.float4_e2m1fn_x4
MULT = mybir.AluOpType.mult
ADD = mybir.AluOpType.add
SIGMOID = mybir.ActivationFunctionType.Sigmoid

P = 128
PACK = 4
ROWS = 4
CHUNK = 512
CHUNKS = J // CHUNK
TILES = N // P
HALF = N // 2
QUANT = 256
LIST_COLS = J // 16
OWN = (2, 1, 1, 1, 1, 1, 1, 4)
TURNED = (1, 1, 1, 1, 1, 0, 2)
LAG = 2
SCALE_ROWS_AT = (96, 112)
KIB = 1024
ALIGN = 64


def tile_list_engram_qf_sigL_kernel(
    tc, tab_words, tab_scales, wk_words, wk_scales, wv8, wv4_words, wv4_scales, st, rT, offs, out
):
    nc = tc.nc
    with ExitStack() as ctx:
        held = ctx.enter_context(tc.tile_pool(name="held", bufs=1))
        front = ctx.enter_context(tc.tile_pool(name="front", bufs=1))
        psum = ctx.enter_context(tc.psum_pool(name="psum", bufs=1))

        def tile(shape, dtype, tag):
            return held.tile(shape, dtype, name=tag, tag=tag, align_bytes=ALIGN)

        def placed(shape, dtype, tag, offset):
            return front.tile(shape, dtype, name=tag, tag=tag, align_bytes=ALIGN, offset=offset)

        offsets = held.tile([P, LIST_COLS], U16, name="offsets")
        nc.sync.dma_start(offsets[:], offs)

        tab_s = placed([P, T], U8, "tab_s", 136 * KIB)
        nc.sync.dma_start(
            out=tab_s[SCALE_ROWS_AT[0] :, :].bitcast(I32), in_=tab_scales.rearrange("a q t -> (a q) t").bitcast(I32)
        )
        nc.vector.memset(tab_s[: SCALE_ROWS_AT[0], :].bitcast(I32), 0)
        tab_w = placed([P, T], U32, "tab_w", 8 * KIB)
        nc.sync.dma_start(out=tab_w[:].bitcast(I32), in_=tab_words[0].rearrange("p t b -> p (t b)").bitcast(I32))

        v_s = [tile([P, J], U8, f"v_s{a}") for a in range(2)]
        for plane in v_s:
            for words in (slice(0, J // 8 + 1), slice(J // 8 + 1, J // 4)):
                nc.vector.memset(plane[:].bitcast(I32)[:, words], 0)
        wk_s = tile([P, 2, N], U8, "wk_s")
        nc.gpsimd.memset(wk_s[:].rearrange("p a n -> p (a n)").bitcast(I32), 0)
        wv4_s = tile([P, N], U8, "wv4_s")
        nc.gpsimd.memset(wv4_s[:].bitcast(I32), 0)

        for r in range(ROWS):
            nc.gpsimd.dma_start(
                out=wk_s[r:P:32, :, :].bitcast(I32),
                in_=wk_scales[:, r:16:ROWS, :].rearrange("a q n -> q a n").bitcast(I32),
            )
        for r in range(ROWS):
            nc.gpsimd.dma_start(out=wv4_s[r:P:32, :].bitcast(I32), in_=wv4_scales[0, r:16:ROWS, :].bitcast(I32))

        state_at = [k * KIB for k in (138, 24, 56, 80, 104, 146, 0, 32)]
        record_at = [k * KIB for k in (0, 32, 64, 88, 112, 154, 40, 64)]

        def load_st(i):
            state = placed([P, J], F32, f"state{i}", state_at[i])
            nc.sync.dma_start(out=state[:], in_=st[i * P : (i + 1) * P, :])
            return state[:]

        def load_record(i):
            record = placed([P, T], F32, f"record{i}", record_at[i])
            nc.sync.dma_start(out=record[:], in_=rT[i * P : (i + 1) * P, :])
            return record

        raw = placed([P, PACK, N], F32, "raw", 146 * KIB)
        nc.sync.dma_start(out=raw[:], in_=wv8.rearrange("(p i) n -> p i n", i=PACK))

        wv4_w = placed([P, 2 * N], U8, "wv4_w", 132 * KIB)
        nc.sync.dma_start(out=wv4_w[:].bitcast(I32), in_=wv4_words[0].bitcast(I32))

        picked_s = placed([P, J], U8, "picked_s", 127 * KIB)
        nc.vector.tensor_copy(picked_s[:], tab_s[:].indirect(offsets[:]))

        def move_scales(a, r):
            nc.sync.dma_start(
                out=v_s[a][r:P:32, :].bitcast(I32),
                in_=picked_s[SCALE_ROWS_AT[a] + r : SCALE_ROWS_AT[a] + 16 : ROWS, :].bitcast(I32),
            )

        def load_key_words(h, offset):
            words = placed([P, 2, HALF], U32, f"wk_w{h}", offset)
            nc.sync.dma_start(
                out=words[:].bitcast(I32),
                in_=wk_words[:, :, h * HALF : (h + 1) * HALF, :].rearrange("a p n b -> p a (n b)").bitcast(I32),
            )
            return words

        moves = [(a, r) for a in range(2) for r in range(ROWS)]
        for a, r in moves[:ROWS]:
            move_scales(a, r)
        wk_w = [load_key_words(0, 134 * KIB)]
        state = load_st(0)
        for a, r in moves[ROWS:]:
            move_scales(a, r)

        wv8_s = tile([P, N], U8, "wv8_s")
        wv8_w = tile([P, N], U32, "wv8_w")

        grouped = placed([P, N, PACK], BF16, "grouped", 48 * KIB)

        def quantize(cols):
            nc.vector.quantize_mx(
                out=wv8_w[:, cols].bitcast(FP8X4),
                scales=wv8_s[:, cols],
                in_=grouped[:, cols, :].rearrange("p n i -> p (n i)"),
            )

        for n0 in range(0, HALF, QUANT):
            cols = slice(n0, n0 + QUANT)
            nc.scalar.copy(grouped[:, cols, :], raw[:, :, cols].rearrange("p i n -> p n i"))
            quantize(cols)

        v_w = tile([P, 2, 2 * J], U8, "v_w")
        step = LIST_COLS // CHUNKS
        picked_w = []
        for c in range(CHUNKS):
            picked = placed([P, CHUNK], U32, f"picked{c}", record_at[c + 1] - KIB)
            nc.vector.tensor_copy(picked[:], tab_w[:].indirect(offsets[:, c * step : (c + 1) * step]))
            picked_w.append(picked)
        for c in range(CHUNKS):
            nc.vector.tensor_copy(
                v_w[:].bitcast(U16)[:, :, c * CHUNK : (c + 1) * CHUNK],
                picked_w[c][:].bitcast(U16).rearrange("p (j d) -> p d j", d=2),
            )

        nc.vector.tensor_copy(grouped[:, HALF:, :], raw[:, :, HALF:].rearrange("p i n -> p n i"))
        quantize(slice(HALF, N))

        def moving(a, c):
            return dict(
                rhs=v_w[:, a, 2 * c * CHUNK : 2 * (c + 1) * CHUNK].bitcast(FP4X4),
                rhs_scale=v_s[a][:, c * CHUNK : (c + 1) * CHUNK],
            )

        def value_sum(i, c):
            rows = slice(i * P, (i + 1) * P)
            bank = psum.tile([P, CHUNK], F32, name=f"bank{c + CHUNKS * (max(i, 1) % 2)}")
            nc.tensor.matmul_mx(
                out=bank[:],
                lhsT=wv8_w[:, rows].bitcast(FP8X4),
                lhsT_scale=wv8_s[:, rows],
                start=True,
                stop=False,
                **moving(0, c),
            )
            nc.tensor.matmul_mx(
                out=bank[:],
                lhsT=wv4_w[:, 2 * i * P : 2 * (i + 1) * P].bitcast(FP4X4),
                lhsT_scale=wv4_s[:, rows],
                start=False,
                stop=True,
                **moving(1, c),
            )
            return bank

        def key_sum(i, c):
            bank = psum.tile([P, CHUNK], F32, name=f"bank{c + CHUNKS * ((i + 1) % 2)}")
            for a in range(2):
                nc.tensor.matmul_mx(
                    out=bank[:],
                    lhsT=wk_w[i * P // HALF][:, a, i * P % HALF : i * P % HALF + P].bitcast(FP8X4),
                    lhsT_scale=wk_s[:, a, i * P : (i + 1) * P],
                    start=(a == 0),
                    stop=(a == 1),
                    **moving(a, c),
                )
            return bank

        identity = tile([P, P], F32, "identity")
        make_identity(nc, identity[:])

        def add_by_transposes(c, banks, result, gate):
            blocks = [slice(c * CHUNK + b * P, c * CHUNK + (b + 1) * P) for b in range(CHUNK // P)]
            cols = slice(c * CHUNK, (c + 1) * CHUNK)
            turned = psum.tile([P, CHUNK], F32, name=f"bank{banks[0]}")
            for b, block in enumerate(blocks):
                for first, addend in ((True, gate), (False, result)):
                    nc.tensor.matmul(
                        turned[:, b * P : (b + 1) * P],
                        addend[:, block],
                        identity[:],
                        start=first,
                        stop=not first,
                        is_transpose=True,
                    )
            nc.scalar.copy(gate[:, cols], turned[:])
            back = psum.tile([P, CHUNK], F32, name=f"bank{banks[1]}")
            for b, block in enumerate(blocks):
                nc.tensor.transpose(back[:, b * P : (b + 1) * P], gate[:, block], identity[:])
            nc.scalar.copy(result[:, cols], back[:])

        stores = []
        waiting = []
        for i in range(TILES):
            rows = slice(i * P, (i + 1) * P)
            if i > 0:
                state = load_st(i)
            record = load_record(i)
            if i == 2:
                wk_w.append(load_key_words(1, 128 * KIB))

            if i == 0:
                ke = [key_sum(i, c) for c in range(CHUNKS)]
                ve = [value_sum(i, c) for c in range(CHUNKS)]
            else:
                ve = [value_sum(i, c) for c in range(CHUNKS)]
                ke = [key_sum(i, c) for c in range(CHUNKS)]

            last = i == TILES - 1
            own = OWN[i]
            gate = tile([P, J], F32, f"gate{i % 4}")
            if own < CHUNKS:
                value = tile([P, J], F32, f"value{i % 2}")
            for c in range(CHUNKS):
                cols = slice(c * CHUNK, (c + 1) * CHUNK)
                nc.vector.tensor_tensor(state[:, cols], ke[c][:], state[:, cols], MULT)
                nc.scalar.activation(gate[:, cols], state[:, cols], SIGMOID)
            for c in range(own, CHUNKS):
                nc.scalar.copy(value[:, c * CHUNK : (c + 1) * CHUNK], ve[c][:])
            if last:
                for c in range(TURNED[i - 1]):
                    first = CHUNKS * ((i + 1) % 2) + 2 * c
                    add_by_transposes(c, (first, first + 1), *waiting[i - 1])
            elif i >= LAG:
                first = CHUNKS * ((i + 1) % 2)
                for c in range(TURNED[i - LAG]):
                    add_by_transposes(c, (first, first + 1), *waiting[i - LAG])
            waiting.append((state, gate))
            for c in range(own):
                cols = slice(c * CHUNK, (c + 1) * CHUNK)
                nc.vector.tensor_tensor(gate[:, cols], ve[c][:], gate[:, cols], MULT)
            pieces = ((own, 2), (max(own, 2), CHUNKS))
            for c0, c1 in pieces:
                if c0 < c1:
                    cols = slice(c0 * CHUNK, c1 * CHUNK)
                    nc.gpsimd.tensor_tensor(gate[:, cols], value[:, cols], gate[:, cols], MULT)

            result = state
            if not last:
                for h in range(2):
                    nc.vector.tensor_copy(
                        result[:, h * J // 2 : (h + 1) * J // 2],
                        record[:].indirect(offsets[:, 2 * h * step : 2 * (h + 1) * step]),
                    )
                for c0, c1 in ((TURNED[i], 2), (2, CHUNKS)):
                    if c0 < c1:
                        cols = slice(c0 * CHUNK, c1 * CHUNK)
                        nc.gpsimd.tensor_tensor(result[:, cols], result[:, cols], gate[:, cols], ADD)
                stores.append((out[rows, :], result))
            else:
                for dst, src in stores:
                    nc.sync.dma_start(out=dst, in_=src)
                for c in range(CHUNKS):
                    cols = slice(c * CHUNK, (c + 1) * CHUNK)
                    listed = record[:].indirect(offsets[:, c * step : (c + 1) * step])
                    nc.vector.tensor_tensor(result[:, cols], listed, gate[:, cols], ADD)
                    if c > 0:
                        done = slice(0, 2 * CHUNK) if c == 1 else cols
                        nc.scalar.dma_start(out=out[rows, done], in_=result[:, done])
